import numpy as np, ml_dtypes
CORES = [23,119,17,113]
N = 4
BF = ml_dtypes.bfloat16
W, P, R, M0, M, S, RO, TH = 4096, 256, 256, 832, 1856, 3, 2, 700
def even(rng, *shape):
    return rng.integers(0, W - 1, shape)
def uneven(rng, *shape):
    return np.minimum(np.exp2(12 * rng.random(shape)).astype(np.int64) - 1, W - 2)
def edgy(rng, *shape):
    return (rng.random(shape) < 0.4) * (W - 2)
def across(t):
    y = t ^ (W // 2)
    return np.where(y == W - 1, W - 2, y)
def look(rng):
    x = rng.integers(0, 256, (16, W)); h = W // 2; m = rng.choice(np.array([0, 8, 40, 90, 120]), h)
    x[:, h:] = np.clip(x[:, :h] + rng.integers(-m, m + 1, (16, h)), 0, 255)
    return x
def rough(rng):
    return np.minimum((np.exp2(8 * rng.random((1, W))) * rng.random((16, W))).astype(np.int64), 255)
def grow(rng, tok, stem, slots, keep=0):
    k = np.arange(16)[:, None]; o = R + keep + rng.permutation(M0 - R - 2 * keep); h = len(o) // 2
    L = np.full((16, M0), W - 1); ch = np.zeros((16, M0), np.int64); F = tok(rng, 16, M0); e = np.zeros(M0, np.int64)
    levels = [np.arange(R), o[:h], o[h:h + h // 2], o[h + h // 2:]]
    for z in range(3):
        up, dn = levels[z], levels[z + 1]; n = len(dn)
        x = rng.permutation(slots)[:n] if z == 0 else rng.permutation(16 * len(up))[:n]
        p, t = up[x >> 4], x & 15; T = tok(rng, 16, n)
        if z == 0:
            T = np.where(rng.random((16, n)) < 0.8, stem[:, x], T); T[0] = x
        s = e[p]; e[dn] = np.minimum(16, s + rng.choice(np.array([1, 1, 2, 3, 5, 8, 16]), n))
        y = (T & -16) + t; T = np.where(k == s, np.where(y == W - 1, W - 17, y), T)
        F[:, dn] = np.where(k < s, F[:, p], T)
        stray = (rng.random(n) < 0.125) & (rng.random((16, n)) < 0.5) & (k != e[dn])
        L[:, dn] = np.where((k >= s) & (k < e[dn]), T, np.where(stray, tok(rng, 16, n), W - 1)); ch[t, p] = dn
        if z == 0: L[0, dn] = np.where(rng.random(n) < 0.1, tok(rng, n), L[0, dn])
    return L, ch, F
def ask(rng, tok, F):
    k = np.arange(16)[:, None]; q = F[:, rng.integers(R, M0, P)]; z = rng.integers(1, 17, P); near = q ^ (W // 2)
    q = np.where((k > 0) & (rng.random((16, P)) < 0.3) & (near != W - 1), near, q)
    y = tok(rng, 16, P); y = np.where(rng.random((16, P)) < 0.5, (y & -16) + (q & 15), y); y = np.where(y == W - 1, W - 17, y)
    return np.where((k >= z) | (rng.random(P) < 0.125), y, q)
def draw(rng, tok, shape):
    h = (M0 - R) // 2; stem = [tok(rng, 16, W) for g in range(8)]; slots = [rng.permutation(W - 1)[:h + h // 4] for g in range(8)]; d = []
    for r in range(N):
        for g in range(8):
            L, ch, F = grow(rng, tok, stem[g], slots[g]); d.append([shape(rng), L, ch, ask(rng, tok, F)])
    return d
def apart(rng):
    return 16 * rng.permutation(R)[:P] + rng.integers(0, 15, P)
def pack(d):
    a = [np.stack([x[z] for x in d]).reshape(N, 128, -1) for z in range(4)]
    return {"desc": a[0].astype(np.float32).astype(BF), "edge": a[1].astype(np.int32), "child": a[2].astype(np.int32), "req": a[3].astype(np.int32)}
def setup_inputs(rng):
    return pack(draw(rng, even, look))
def setup_inputs_spread(rng):
    return pack(draw(rng, uneven, rough))
def setup_inputs_ends(rng):
    k = np.arange(16)[:, None]; h = (M0 - R) // 2; d = []
    stem = [edgy(rng, 16, W) for g in range(8)]; slots = [2 + rng.permutation(W - 18)[:h + h // 4] for g in range(8)]
    for r in range(N):
        for g in range(8):
            L, ch, F = grow(rng, edgy, stem[g], slots[g], 1)
            x = rng.integers(0, 2, (16, W)) * 255; x[:, 0] = 0; x[:, W - 2] = 255; x[:8, W // 2] = 0; x[8:, W // 2] = 255
            q = np.where(k >= rng.integers(1, 17, P), edgy(rng, 16, P), F[:, rng.integers(R + 1, M0 - 1, P)])
            ch[0, 0] = R; ch[1, 0] = 1; ch[14, R - 1] = M0 - 1
            L[:, R] = 0; L[15, R] = W // 2; L[:, M0 - 1] = 0; L[0, M0 - 1] = W - 2
            q[:, 0] = 0; q[15, 0] = W - 2; q[0, 1] = 1
            q[:, P - 1] = 0; q[0, P - 1] = W - 2; q[15, P - 1] = W - 2
            if g % 2: q[14, P - 1] = W - 2
            d.append([x, L, ch, q])
    return pack(d)
def setup_inputs_corners(rng):
    k = np.arange(16)[:, None]; i = np.arange(P); d = draw(rng, even, look)
    for j in range(8 * N):
        x, L, ch, q = d[j]; z = j % 11; q0 = apart(rng)
        if z in (2, 3, 4, 6, 8, 9, 10):
            ch[:] = 0; L[:] = W - 1
        if z in (9, 10):
            x = np.concatenate([rng.integers(0, 100, (16, W // 2)), rng.integers(156, 256, (16, W // 2))], axis=1)
        if z == 0:
            ch[:] = 0; q[0] = rng.choice(np.array([0, 1, 15, 16, W - 17, W - 2]), P)
            L[:, 0] = np.where(k < 8, q[:, :1], W - 1)[:, 0]
        if z == 1:
            y = int(rng.choice(np.flatnonzero(ch[:, :R].T.reshape(-1)))); e = L[:, ch[y & 15, y >> 4]][:, None]
            q = np.where((rng.random(P) < 0.5) & (k > 0) & (e < W - 1), e, q); q[0] = y
        if z in (2, 3):
            q = even(rng, 16, P); q[0] = q0; u = R + i if z == 2 else q0 >> 4; ch[q0 & 15, q0 >> 4] = u; m = rng.integers(0, 5, P)
            e = np.where(((m == 1) & (k == 15)) | ((m == 2) & (k == 0)) | ((m == 3) & (k == 1)), even(rng, 16, P), q)
            L[:, u] = np.where((m == 4) & (k >= (8 if z == 2 else np.maximum(rng.integers(-5, 16, P), 0))), W - 1, e)
        if z == 4:
            nc = (M0 - R) // 4; T = even(rng, 16, nc); T[0] = rng.permutation(W - 1)[:nc]
            for m in range(4):
                u = R + 4 * np.arange(nc) + m; L[m, u] = T[m]; ch[T[m] & 15, T[0] >> 4 if m == 0 else u - 1] = u
            q = T[:, i % nc]
        if z == 5: L[:] = W - 1
        if z == 6:
            q = even(rng, 16, P); q[0] = q0; w = q0 >> 4; a = np.flatnonzero(w % 2 == 0); ch[q0[a] & 15, w[a]] = w[a] + 1
            L[:, w[a] + 1] = np.where(k < rng.integers(1, 16, len(a)), q[:, a], even(rng, 16, len(a))); q[0] = np.where(w % 4 == 3, q0 - 32, q0)
        if z == 7: q[1:] = rng.choice(np.array([0, 1, W - 3, W - 2]), (15, 1))
        if z == 8:
            nb = P // N; nc = min((M0 - R) // 17, nb); a = rng.permutation(nb)[:nc]; o = nb + rng.permutation(P - nb)[:nc]
            m = rng.integers(2, 16, nc); p = rng.integers(1, m); u = R + 17 * np.arange(nc)
            q = even(rng, 16, P); q[0] = q0; q[:, o] = np.where(k < p, q[:, a], q[:, o]); T = q[:, a]
            h = ((T[1:] * T[:-1]) >> 5) & (W - 1); h = np.concatenate([T[:1], np.where(h == W - 1, 0, h)])
            ch[T[0] & 15, T[0] >> 4] = u; L[:, u] = np.where(k < m, T, W - 1)
            for t in range(16):
                e = m + rng.integers(0, 17 - m); ch[t, u] = u + 1 + t
                L[:, u + 1 + t] = np.where((k >= m) & (k < e), np.where(rng.random((16, nc)) < 0.1, even(rng, 16, nc), h), W - 1)
        if z == 9:
            q = even(rng, 16, P); q[0] = q0; nc = P // 16; n = np.arange(nc); c = R + n; m = rng.integers(1, 8, nc)
            s = np.sort(rng.permutation(np.flatnonzero(q0 > 15))[:9 * nc].reshape(9, nc), axis=0)
            u, o, uu, oo = [q0[s[t]] >> 4 for t in (0, 2, 8, 5)]; T = q[:, s[0]]; y = q[:, s[8]]
            q[:, s[1]] = np.where(k < m, T, np.where(k == m, np.where((T ^ 1) == W - 1, 0, T ^ 1), q[:, s[1]]))
            q[0, s[2:5]] = 16 * o + (rng.integers(0, 15, nc) + 5 * np.arange(3)[:, None]) % 15
            q[0, s[5:8]] = 16 * oo + (rng.integers(0, 15, nc) + 5 * np.arange(3)[:, None]) % 15
            ch[T[0] & 15, u] = c; ch[T[m, n] & 15, c] = o; ch[y[0] & 15, uu] = oo
            L[:, c] = np.where(k < m, T, W - 1); L[:, o] = np.where(k <= m, T, across(T))
            L[:, oo] = np.where(k < rng.integers(1, 16, nc), y, W - 1)
        if z == 10:
            q = even(rng, 16, P); q[0] = q0; ch[q0 & 15, q0 >> 4] = R + i; p = rng.integers(1, 16, P); y = across(q)
            y = np.where(rng.random(P) < 0.25, y, (y & -16) + rng.integers(0, 15, P))
            L[:, R + i] = np.where(k == p, y, q)
        d[j] = [x, L, ch, q]
    return pack(d)
def setup_inputs_ties(rng):
    k = np.arange(16)[:, None]; i = np.arange(P); h = 3 * P // 4; s = np.where(i < h, i, i - P // 2); d = []
    for j in range(8 * N):
        x = look(rng); b = 16 * rng.integers(0, R - 1, 16) + np.arange(16)
        A = rng.permutation(W - 1); A = A[~np.isin(A, b)][:P]; B = b[np.where(rng.random(P) < 0.25, A & 15, rng.integers(0, 16, P))]; p = rng.integers(1, 16, P)
        x[:, b] = rng.integers(100, 121, (16, 16)); y = TH + rng.integers(-1, 2, P); v = rng.integers(-20, 21, (8, P))
        D = (y >> 4) + (k < (y & 15)) + np.concatenate([v, -v])
        f1 = rng.integers(0, 16, P); f2 = f1 ^ (1 << rng.integers(0, 4, P)); w = np.where(y > TH, 257, 259); z = y - w; o = k - (k > f1) - (k > f2)
        D = np.where(rng.random(P) < 0.5, D, np.where(k == f1, w >> 1, np.where(k == f2, w - (w >> 1), z // 14 + (o < z % 14))))
        x[:, A] = x[:, B] + D * np.where(D > 100, 1, rng.choice(np.array([-1, 1]), (16, P)))
        T = even(rng, 16, P); T[0] = apart(rng); T = T[:, s]
        L = np.full((16, M0), W - 1); ch = np.zeros((16, M0), np.int64)
        L[:, R:R + h] = np.where(k == p, A, T)[:, :h]; ch[T[0] & 15, T[0] >> 4] = R + s
        d.append([x, L, ch, np.where(k == p, B, T)])
    return pack(d)
def check_inputs(d):
    bad = []
    for a, lo, hi in (("desc", 0, 255), ("edge", 0, W - 1), ("child", 0, M0 - 1), ("req", 0, W - 2)):
        x = np.asarray(d[a]).astype(np.float64)
        if not (np.min(x) >= lo and np.max(x) <= hi): bad.append("range of " + a)
        if np.any(x != np.floor(x)): bad.append("whole numbers in " + a)
    c = np.sort(np.asarray(d["child"]).reshape(N, 8, 16 * M0), axis=-1)
    if np.any((c[..., 1:] == c[..., :-1]) & (c[..., 1:] > 0)): bad.append("a node stands twice in child")
    return bad
def walk(X, L, C, Q, rnd):
    i = np.arange(P); k = np.arange(16)[:, None]; n = M0 + 2 * P * rnd + 2 * i
    v = Q[0] >> 4; a = np.zeros(P, np.int64); on = np.ones(P, bool)
    for step in range(S):
        low = np.full(M, P); np.minimum.at(low, v[on], i[on])
        act = on & (low[v] == i)
        t = Q[np.minimum(a, 15), i] & 15; c = C[t, v]; E = L[:, c]; none = E == W - 1
        dist = np.add.reduce(np.abs(X[:, E] - X[:, Q]), axis=0)
        b = np.min(np.where((k >= a) & none, k, 16), axis=0)
        l = np.min(np.where((k >= a) & (none | (dist > TH)), k, 16), axis=0)
        leaf = act & ((c == 0) | ((l == a) & (l < b)))
        down = act & (c > 0) & (l == b)
        cut = act & (c > 0) & (l > a) & (l < b) & (low[c] == P)
        j = np.flatnonzero(cut); lj = l[j]; cj = c[j]; ej = E[lj, j]; qj = Q[lj, j]
        f = np.unique(qj, return_index=True)[1]
        X[:, qj[f]] = (X[:, qj[f]] + X[:, ej[f]]) >> 1
        L[:, n[j]] = np.where(k >= lj, E[:, j], W - 1); C[:, n[j]] = C[:, cj]
        L[:, cj] = np.where(k < lj, E[:, j], W - 1); C[:, cj] = 0; C[ej & 15, cj] = n[j]
        two = (ej & 15) != (qj & 15); o = j[two]
        C[qj[two] & 15, cj[two]] = n[o] + 1; L[:, n[o] + 1] = np.where(k >= l[o], Q[:, o], W - 1)
        j = np.flatnonzero(leaf)
        L[:, n[j]] = np.where(k >= a[j], Q[:, j], W - 1); C[t[j], v[j]] = n[j]
        v = np.where(down, c, v); a = np.where(down, b, a); on = on & ~leaf & ~cut & (a < 16)
    return a
def reference(desc, edge, child, req):
    X = desc.astype(np.float32).astype(np.int64).reshape(N, 8, 16, W); Q = req.astype(np.int64).reshape(N, 8, 16, P)
    L = np.full((N, 8, 16, M), W - 1); L[..., :M0] = edge.reshape(N, 8, 16, M0)
    C = np.zeros((N, 8, 16, M), np.int64); C[..., :M0] = child.reshape(N, 8, 16, M0)
    k = np.arange(1, 16)[:, None]; B = P // N
    for rnd in range(RO):
        new = np.zeros_like(Q)
        for r in range(N):
            for g in range(8):
                q = Q[r, g]; a = walk(X[r, g], L[r, g], C[r, g], q, rnd)
                h = ((q[1:] * q[:-1]) >> 5) & (W - 1); h = np.where(h == W - 1, 0, h)
                q = np.concatenate([q[:1], np.where(k >= a, h, q[1:])])
                for e in range(N): new[(r + e) % N, g, :, e * B:(e + 1) * B] = q[:, e * B:(e + 1) * B]
        Q = new
    return {"yd": X.reshape(N, 128, W).astype(np.float32).astype(BF), "ye": L.reshape(N, 128, M).astype(np.float32), "yr": Q.reshape(N, 128, P).astype(np.float32)}

@@ -1,0 +1,597 @@
+from concourse.bass import DstId, RemoteDMATransfer
+from concourse.mybir import AluOpType, ActivationFunctionType
+
+A_ = AluOpType
+F_ = ActivationFunctionType
+BF, HF, FF, II, UU = "bfloat16", "float16", "float32", "int32", "uint16"
+SCRATCH = {}
+MATS = ["B", "I", "TR", "U", "TS", "NI", "NB", "N16", "R0", "R016", "HALF", "BN4", "TRN4K", "TRP4K", "BN4K", "BP4K",
+        "IN4K", "I2K", "SH", "NSH", "IR", "K6", "K10", "K18", "BN1K", "K1", "K20"] + ["S%d" % f for f in range(16)]
+
+
+def _decl():
+    def sb(w, d, *names):
+        for n in names:
+            SCRATCH[n] = ("sbuf", [128, w], d)
+    sb(4368, BF, "D"), sb(2112, FF, "E", "C", "OCT"), sb(4096, BF, "XQ", "DF"), sb(2048, BF, "XL"), sb(4096, HF, "EQA")
+    sb(128 * len(MATS), BF, "cm")
+    sb(832, II, "ein", "cin"), sb(256, II, "qin", "XI", "HP", "HH")
+    sb(256, UU, "QU", "QN", "LQ1", "LU")
+    sb(256, HF, "QC0", "QH0", "QC1", "QH1", "VB", "P16", "BAD", "NN", "CQ", "CL", "EV", "LC", "LH", "QB", "TP", "DG",
+       "R1A", "R1B", "R2A", "W1", "W2", "W2G", "OT", "NA0", "NB0", "NA1", "NB1", "DIAG")
+    sb(256, BF, "ONES", "OA", "KA", "GS", "ACT", "OCC", "CO", "DO", "LO", "FO", "DW", "XG", "XH", "CW")
+    sb(256, FF, "CV", "CC", "VA", "VBB", "VC", "EC", "QF", "HM", "HT", "HD", "HR", "HQ", "ST", "YRL", "YRO", "i256", "nb")
+    sb(16, UU, "vl", "cu", "ql", "ll", "yel", "ycl", "yxl", "ysl")
+    sb(16, FF, "vs", "cf", "dum", "dumx", "vmd", "cmd", "p1", "p2", "ye2", "yc2", "qs", "x1", "qmd", "px", "yx2", "ps", "ys2")
+    sb(128, FF, "im", "ih", "il", "IF"), sb(128, BF, "sl"), sb(8, FF, "gi", "pf", "pm", "pv", "p0", "save"), sb(8, II, "pi", "pj", "pd")
+    sb(8, BF, "g8"), sb(16, BF, "savd")
+    for b in range(8):
+        SCRATCH["b%d" % b] = ("psum", [128, 512], FF)
+
+
+_decl()
+SEMAPHORES = ["qv", "qs", "qt", "qg"] + ["d%d" % i for i in range(9)] + ["ls0", "ls1", "ar0", "ar1"]
+
+
+def tracker(g, T):
+    eng = {"v": g.vector, "s": g.scalar, "t": g.tensor, "g": g, "y": g.sync}
+    obs = {q: {} for q in eng}
+    cnt, snap, acc, bank, tot = {}, {}, {}, {}, {}
+
+    def sem(pq):
+        return T.sem["q" + pq] if pq in eng else T.sem[pq]
+
+    def clash(a, b):
+        if a[1] <= b[0] or b[1] <= a[0]:
+            return False
+        return not (a[2] == b[2] > 1 and (a[0] - b[0]) % a[2])
+
+    def learn(q, pq, n):
+        o = obs[q]
+        if o.get(pq, 0) >= n:
+            return
+        o[pq] = n
+        for k, m in snap.get((pq, n), {}).items():
+            if o.get(k, 0) < m:
+                o[k] = m
+
+    def waits(q, reads, writes):
+        req = {}
+        for w, regs in ((0, reads), (1, writes)):
+            for nm, lo, hi, st in regs:
+                if SCRATCH[nm][0] == "psum":
+                    for pq, n in bank.get(nm, {}).items():
+                        if pq != q:
+                            req[pq] = max(req.get(pq, 0), n)
+                    continue
+                for r, pq, n, pw in acc.get(nm, []):
+                    if not (w or pw) or not clash(r, (lo, hi, st)):
+                        continue
+                    req[pq] = max(req.get(pq, 0), n)
+        for pq in sorted(req, key=lambda k: -req[k]):
+            if obs[q].get(pq, 0) < req[pq]:
+                eng[q].wait_ge(sem(pq), req[pq])
+                learn(q, pq, req[pq])
+
+    def note(pq, n, reads, writes, issuer):
+        snap[(pq, n)] = dict(obs[issuer]) if issuer else {}
+        for w, regs in ((0, reads), (1, writes)):
+            for nm, lo, hi, st in regs:
+                if SCRATCH[nm][0] == "psum":
+                    bank[nm] = {pq: n}
+                    continue
+                keep = []
+                for e in acc.get(nm, []):
+                    r = e[0]
+                    inside = lo <= r[0] and r[1] <= hi and (st == 1 or r == (lo, hi, st))
+                    if not (inside and (w or (e[1] == pq and not e[3]))):
+                        keep.append(e)
+                acc[nm] = keep + [((lo, hi, st), pq, n, w)]
+
+    def op(q, fn, reads, writes):
+        waits(q, reads, writes)
+        n = cnt.get(q, 0) + 1
+        cnt[q] = tot[q] = n
+        fn(eng[q]).then_inc(sem(q), 1)
+        note(q, n, reads, writes, q)
+
+    def dma(q, name, out, in_, reads, writes):
+        waits(q, reads, writes)
+        eng[q].dma_start(out, in_).then_inc(T.sem[name], 16)
+        tot[name] = 16
+        note(name, 16, reads, writes, q)
+
+    def finish(q):
+        for pq, n in tot.items():
+            if obs[q].get(pq, 0) < n:
+                eng[q].wait_ge(sem(pq), n)
+                learn(q, pq, n)
+    return op, dma, waits, note, tot, finish
+
+
+def rank_program(g, core, T, topo):
+    rank = T.rank_of(core)
+    if rank is None:
+        return
+    NR = len(T.cores)
+    op, dma, waits, note, tot, finish = tracker(g, T)
+
+    def X(nm, lo=0, hi=None, st=1):
+        hi = SCRATCH[nm][1][1] if hi is None else hi
+        return (T[nm][:, lo:hi:st] if st > 1 else T[nm][:, lo:hi], [(nm, lo, hi, st)])
+
+    def IND(win, off):
+        return (win[0].indirect(off[0]), win[1] + off[1])
+
+    def O(x):
+        return X(x) if isinstance(x, str) else x
+
+    def tt(out, a, b, f):
+        out, a, b = O(out), O(a), O(b)
+        op("v", lambda e: e.tensor_tensor(out[0], a[0], b[0], f), a[1] + b[1], out[1])
+
+    def ts(out, a, s1, f1, s2=None, f2=None):
+        out, a = O(out), O(a)
+        r, v1 = list(a[1]), s1
+        if isinstance(s1, tuple):
+            v1 = s1[0]
+            r = r + s1[1]
+        if f2 is None:
+            op("v", lambda e: e.tensor_scalar(out[0], a[0], v1, None, f1), r, out[1])
+        else:
+            op("v", lambda e: e.tensor_scalar(out[0], a[0], v1, s2, f1, f2), r, out[1])
+
+    def cp(out, a):
+        out, a = O(out), O(a)
+        op("v", lambda e: e.tensor_copy(out[0], a[0]), a[1], out[1])
+
+    def fill(out, c):
+        out = O(out)
+        op("v", lambda e: e.memset(out[0], c), [], out[1])
+
+    def act(out, a, f, scale=1.0, bias=0.0):
+        out, a = O(out), O(a)
+        op("s", lambda e: e.activation(out[0], a[0], f, bias=bias, scale=scale), a[1], out[1])
+
+    def iota(out, pat, base, cm):
+        out = O(out)
+        op("g", lambda e: e.iota(out[0], pat, base, cm, allow_small_or_imprecise_dtypes=True), [], out[1])
+
+    def M(nm):
+        j = MATS.index(nm)
+        return X("cm", 128 * j, 128 * j + 128)
+
+    def mm(out, m, rhs, start=False, stop=False):
+        m, rhs = (M(m) if isinstance(m, str) else m), O(rhs)
+        op("t", lambda e: e.matmul(out[0], m[0], rhs[0], start, stop), m[1] + rhs[1], out[1])
+
+    def mms(out, *pairs):
+        for j, (m, rhs) in enumerate(pairs):
+            mm(out, m, rhs, j == 0, j == len(pairs) - 1)
+
+    def wrap(out, src):
+        for f in range(16):
+            mm(out, "S%d" % f, X(src, f, 256, 16), f == 0, f == 15)
+
+    def P(b, h):
+        return X("b%d" % b, 256 * h, 256 * h + 256)
+
+    dma("y", "d0", T.qin[:], T.req[:], [], [("qin", 0, 256, 1)])
+    dma("s", "d1", T.cin[:], T.child[:], [], [("cin", 0, 832, 1)])
+    dma("y", "d8", T.savd[:], T.desc[:, 4080:4096], [], [("savd", 0, 16, 1)])
+    dma("y", "d2", T.D[:, 0:4080], T.desc[:, 0:4080], [], [("D", 0, 4080, 1)])
+    dma("s", "d3", T.ein[:], T.edge[:], [], [("ein", 0, 832, 1)])
+
+    iota("pi", [[0, 8]], 0, 1)
+    iota("ih", [[1, 8], [0, 16]], 0, 0)
+    iota("im", [[1, 128]], 0, 0)
+    iota("gi", [[1, 8]], 0, 0)
+    iota("il", [[0, 8], [1, 16]], 0, 0)
+    iota("dum", [[16, 16]], 1856, 0)
+    iota(X("C", 832, 2112), [[0, 1280]], 0, 0)
+    iota("i256", [[0, 16], [1, 16]], 0, 0)
+    iota(X("E", 832, 2112), [[0, 1280]], 4095, 0)
+    iota("nb", [[2, 256]], 832 - 2048, 0)
+    iota("OCT", [[0, 2112]], 0, 0)
+    PM, PV, PF, P0 = X("pm", 0, 1), X("pv", 0, 1), X("pf", 0, 1), X("p0", 0, 1)
+    fill("ONES", 1.0)
+    s0 = 128 * MATS.index("S0")
+    fill(X("cm", s0, s0 + 2048), 0.0)
+    fill(X("D", 4096, 4368), 1000.0)
+    ts("pj", "pi", 15, A_.bitwise_and)
+    ts("pd", "pi", 4, A_.logical_shift_right)
+    cp("pf", "pi")
+    cp("pm", "pj")
+    cp("pv", "pd")
+    ts("p0", "pj", 0.0, A_.is_equal)
+    ts(M("B"), "ih", PV, A_.is_equal)
+    ts(M("I"), "im", PF, A_.is_equal)
+    ts("g8", "gi", PV, A_.is_equal)
+    ts(M("R0"), M("B"), P0, A_.mult)
+    for nm, a, s in (("R016", "R0", -16.0), ("K18", "I", 20480.0), ("N16", "I", -16.0), ("NI", "I", -1.0), ("NB", "B", -1.0)):
+        act(M(nm), M(a), F_.Copy, s)
+    for f in range(16):
+        if f % 2:
+            cp(X("cm", s0 + 129 * f, s0 + 128 * f + 128, 16), "g8")
+        else:
+            act(X("cm", s0 + 129 * f, s0 + 128 * f + 128, 16), "g8", F_.Copy)
+    ts("sl", "il", PM, A_.is_ge)
+    for nm, a, s in (("K20", "I", 1048576.0), ("HALF", "I", 0.5), ("BN4", "B", -4.0), ("BN4K", "B", -4096.0), ("BP4K", "B", 4096.0),
+                     ("IN4K", "I", -4096.0), ("I2K", "I", 2048.0), ("K6", "I", 6144.0), ("K10", "I", 10240.0), ("BN1K", "B", -1024.0),
+                     ("K1", "I", 1024.0)):
+        act(M(nm), M(a), F_.Copy, s)
+
+    def late_consts():
+        tt(M("TR"), "sl", M("B"), A_.mult)
+        ts("DIAG", "i256", PM, A_.is_equal)
+        tt(M("TS"), M("TR"), M("I"), A_.subtract)
+        tt(M("U"), M("TS"), M("I"), A_.subtract)
+        ts("dumx", "dum", 4112.0 - 1856.0, A_.add)
+        ts("IF", "im", PF, A_.is_equal)
+        ts(M("SH"), "im", PF, A_.subtract, 1.0, A_.is_equal)
+        tt(M("SH"), M("SH"), M("B"), A_.mult)
+        tt(M("IR"), M("I"), M("R0"), A_.mult)
+        tt(M("IR"), M("I"), M("IR"), A_.subtract)
+        ts(M("NSH"), M("SH"), -1.0, A_.mult)
+        ts(M("TRN4K"), M("TR"), -4096.0, A_.mult)
+        ts(M("TRP4K"), M("TR"), 4096.0, A_.mult)
+        for j, nm in enumerate(("NA0", "NB0", "NA1", "NB1")):
+            ts(nm, "nb", float(j % 2 + 512 * (j // 2)), A_.add)
+
+    WD, WDS = X("D", 0, 4112), X("D", 0, 4368)
+    WC, WE, WCS, WES = X("C", 0, 1856), X("E", 0, 1856), X("C"), X("E")
+    W0 = X("b6", 0, 16)
+
+    def prep(src, qc, qh):
+        ts(qc, src, -2048.0, A_.add)
+        ts(qh, src, 1.0 / 16, A_.mult, 1152 - 0.46875, A_.add)
+
+    def lists():
+        wrap(W0, "VB")
+        ts("vl", W0, 1855.0, A_.min)
+        ts("vs", W0, 1.0 / 16, A_.mult)
+
+    def roots(qc, qh):
+        mms(P(7, 0), ("R0", qh))
+        mms(P(7, 1), ("R0", qc), ("R016", qh), ("K18", "ONES"))
+        ts("VB", P(7, 0), -1152.0, A_.add, 1.0 / 16, A_.mult)
+        ts("OT", P(7, 1), PM, A_.is_equal, 1.0 / 16, A_.mult)
+        lists()
+        ts("OA", "ONES", P0, A_.mult)
+        fill("KA", 1.0)
+
+    def qres(qc, qh):
+        mms(P(1, 0), ("I", qc))
+        mms(P(1, 1), ("I", qc), ("N16", qh), ("K18", "ONES"))
+
+    def lh():
+        ts("LC", "LU", -2048.0, A_.add)
+        ts("LH", "LU", 1.0 / 16, A_.mult, 1152 - 0.46875, A_.add)
+
+    def lres():
+        mms(P(2, 0), ("I", "LC"))
+        mms(P(2, 1), ("I", "LC"), ("N16", "LH"), ("K18", "ONES"))
+
+    def gq(c, lst):
+        act(X("XQ", 1024 * c, 1024 * c + 1024), IND(WD, X(lst, 64 * c, 64 * c + 64)), F_.Copy)
+
+    def gl(c):
+        act(X("XL", 1024 * (c - 2), 1024 * (c - 1)), IND(WD, X("LU", 64 * c, 64 * c + 64)), F_.Copy)
+
+    def diffs(c, banks):
+        for h, b in enumerate(banks):
+            lo = 1024 * c + 512 * h
+            mms(X("b%d" % b), ("I", X("XL", lo - 2048, lo - 1536)), ("NI", X("XQ", lo, lo + 512)))
+
+    def mags(c, banks):
+        for h, b in enumerate(banks):
+            lo = 1024 * c + 512 * h
+            act(X("DF", lo, lo + 512), X("b%d" % b), F_.Abs)
+
+    def sub(c):
+        sl = X("DF", 1024 * c, 1024 * c + 1024)
+        tt(sl, IND(WD, X("LU", 64 * c, 64 * c + 64)), X("XQ", 1024 * c, 1024 * c + 1024), A_.subtract)
+
+    def mag(c):
+        sl = X("DF", 1024 * c, 1024 * c + 1024)
+        act(sl, sl, F_.Abs)
+
+    def dist(c):
+        o = X("b0", 64 * c, 64 * c + 64)
+        mm(o, "K20", X("KA", 64 * c, 64 * c + 64), True, False)
+        for k in range(16):
+            mm(o, "S%d" % k, X("DF", 1024 * c + k, 1024 * c + 1024, 16), False, k == 15)
+
+    def causal(cols, code, scal):
+        for c in cols:
+            ts(X("EQA", 256 * c, 512 * c + 256 - 272 * c), X(code, 16 * c, 256), X(scal, c, c + 1), A_.is_equal)
+
+    def count(cols):
+        for c in cols:
+            if c < 15:
+                mm(X("b6", 256 + 16 * (c + 1), 512), "B", X("EQA", 256 * c + 16, 512 * c + 256 - 272 * c))
+
+    def diag():
+        for c in range(16):
+            mm(X("b3", 16 * c, 16 * c + 16), "TS", X("EQA", 256 * c, 256 * c + 16), True, True)
+
+    def diag_add():
+        tt("DG", P(3, 0), "DIAG", A_.mult)
+        mm(P(6, 1), "B", "DG", False, True)
+
+    def child():
+        tt("P16", IND(WC, X("vl")), "OT", A_.mult)
+        wrap(W0, "P16")
+        mms(P(7, 1), ("B", "P16"), ("NI", "VB"))
+
+    def edge():
+        ts("cu", W0, 16.0, A_.mult)
+        cp("LU", IND(WE, X("cu")))
+
+    def cmd():
+        ts("cf", "cu", 1.0, A_.mult)
+        tt("cmd", "cf", "dum", A_.subtract)
+
+    def acts():
+        ts("ACT", P(6, 1), 0.0, A_.min, -1.0 / 16, A_.mult)
+        cp("GS", P(6, 1))
+        wrap(X("b7", 0, 16), "ACT")
+
+    def stamp(n):
+        iota("ST", [[0, 256]], n, 0)
+        ts("vmd", "vs", 16.0, A_.mult)
+        tt("vmd", "vmd", "dum", A_.subtract)
+        tt("ps", "vmd", X("b7", 0, 16), A_.mult)
+        tt("ys2", "ps", "dum", A_.add)
+        cp("ysl", "ys2")
+        cp(IND(X("OCT"), X("ysl")), "ST")
+
+    def gates(n):
+        ts("OCC", IND(X("OCT", 0, 1856), X("cu")), float(n), A_.is_ge)
+        mm(P(3, 0), "I", "OCC")
+
+    def gates2():
+        mm(P(3, 0), "I", "GS", True, False)
+        mm(P(3, 0), "NI", "KA")
+        mm(P(3, 0), "I", "OA")
+        mm(P(5, 0), "I", "GS", True, False)
+        mm(P(5, 0), "NI", "OA")
+        mm(P(4, 0), "I", "GS", True, False)
+
+    def hash_prep(lst, qc):
+        cp("QF", lst)
+        mms(P(0, 1), ("SH", qc), ("I2K", "ONES"))
+        tt("HP", "QF", P(0, 1), A_.mult)
+        ts("HH", "HP", 5, A_.logical_shift_right, 4095, A_.bitwise_and)
+        ts("HM", "HH", 4095.0, A_.is_equal, -4095.0, A_.mult)
+        tt("HT", "HH", "HM", A_.add)
+        tt("HD", "HT", "QF", A_.subtract)
+
+    def send(i, src, dst):
+        used, tr, nls = set(), [], 0
+        peers = [(e, T.cores[(rank + e) % NR]) for e in range(1, NR)]
+        for e, c in sorted(peers, key=lambda x: len(topo.engines(core, x[1]))):
+            es = [k for k in topo.engines(core, c) if k not in used][:4]
+            used.update(es)
+            nls += len(es)
+            rid, pid = topo.addr(c)[0], topo.addr(c)[1]
+            tr.append(RemoteDMATransfer(dst_ids=[DstId(rid=rid, pnc=pid)], dma_engine_mask=sum(1 << k for k in es), remote_sem=T.sem["ar%d" % i],
+                                        src=T[src][:, 64 * e:64 * e + 64], dst=T[dst][:, 64 * e:64 * e + 64]))
+        reg = [(src, 64, 256, 1)]
+        waits("g", reg, [])
+        g.remote_dma_fused(tr, local_sem=T.sem["ls%d" % i])
+        tot["ls%d" % i] = nls
+        note("ls%d" % i, nls, reg, [], "g")
+        tot["ar%d" % i] = 4 * (NR - 1)
+        note("ar%d" % i, 4 * (NR - 1), [], [(dst, 64, 256, 1)], None)
+
+    def leave(rnd):
+        tt("HR", P(4, 0), "HD", A_.mult)
+        if rnd == 0:
+            tt("HQ", "HR", P(7, 1), A_.add)
+            cp("QN", "HQ")
+            send(0, "QN", "LQ1")
+            cp(X("LQ1", 0, 64), X("QN", 0, 64))
+        else:
+            tt("YRO", "HR", P(7, 1), A_.add)
+            send(1, "YRO", "YRL")
+            dma("y", "d4", T.yr[:, 0:64], T.YRO[:, 0:64], [("YRO", 0, 64, 1)], [])
+
+    def walk(rnd, s, lst, qc):
+        n, first = 3 * rnd + s + 1, rnd == 0 and s == 0
+        child()
+        causal(range(0, 8), "VB", "vs")
+        act("CV", IND(WC, X("vl")), F_.Copy)
+        if first:
+            late_consts()
+            cp(X("E", 0, 832), "ein")
+            cp("save", X("E", 0, 8))
+            fill(X("E", 0, 1), 4096.0)
+        edge()
+        mm(P(6, 1), "NB", "OA", True, False)
+        count(range(0, 8))
+        if s == 0:
+            hash_prep(lst, qc)
+        if first:
+            causal(range(8, 16), "VB", "vs")
+            count(range(8, 16))
+            diag()
+            lh()
+            cmd()
+            diag_add()
+            for c in range(4):
+                sub(c)
+                if c == 0:
+                    acts()
+                mag(c)
+                dist(c)
+                if c == 2:
+                    stamp(n)
+                    gates2()
+                    lres()
+            gates(n)
+        else:
+            gl(2)
+            sub(0)
+            gl(3)
+            diffs(2, (4, 5))
+            causal(range(8, 16), "VB", "vs")
+            count(range(8, 16))
+            diag()
+            mags(2, (4, 5))
+            lh()
+            cmd()
+            diag_add()
+            sub(1)
+            diffs(3, (3, 5))
+            lres()
+            acts()
+            mag(0)
+            dist(0)
+            mags(3, (3, 5))
+            dist(2)
+            stamp(n)
+            mag(1)
+            dist(3)
+            gates2()
+            dist(1)
+            gates(n)
+
+    def decide(rnd, s, lst, qc):
+        base, last = 832 + 512 * rnd, s == 2
+        fin = last and rnd == 1
+        ts("BAD", P(0, 0), 1048576.0 + 700.5, A_.is_gt)
+        ts("NN", P(0, 0), 1048576.0 + 200000.0, A_.is_gt)
+        mm(P(3, 0), "U", "BAD")
+        mm(P(3, 0), "I", "NN", False, True)
+        act("CO", P(3, 0), F_.Relu, -1.0, -2.0)
+        mms(P(0, 1), ("U", "BAD"), ("I", "NN"))
+        act("FO", P(0, 1), F_.Relu, -1.0)
+        tt("CQ", "CO", P(1, 0), A_.mult)
+        mm(P(5, 0), "NI", "BAD")
+        mm(P(5, 0), "I", "NN", False, True)
+        act("LO", P(5, 0), F_.Relu, -1.0, -2.0)
+        mm(P(4, 0), "U", "BAD")
+        mm(P(4, 0), "NI", "NN", False, True)
+        act("DO", P(4, 0), F_.Relu, -1.0, -2.0)
+        mms(P(3, 1), ("B", "CQ"))
+        wrap(W0, "CQ")
+        wrap(X("b6", 16, 32), "CO")
+        mms(P(0, 1), ("B", "FO"), ("I", "GS"))
+        act("DW", P(0, 1), F_.Relu, -1.0)
+        if not fin:
+            act("CC", IND(WC, X("cu")), F_.Copy)
+        tt("CL", "CO", P(2, 0), A_.mult)
+        tt("R1A", "CO", P(2, 1), A_.mult)
+        tt("R2A", "CO", P(1, 1), A_.mult)
+        cp("QB", P(3, 1))
+        ts("x1", X("b6", 16, 32), -5000.0, A_.mult, 5000.0, A_.add)
+        tt("qs", "x1", W0, A_.add)
+        ts("ql", W0, 2048.0, A_.add)
+        act("XG", IND(WD, X("ql")), F_.Copy)
+        if last:
+            mms(P(7, 1), ("I", qc), ("I2K", "ONES"))
+        wrap(X("b7", 0, 16), "CL")
+        causal(range(0, 16), "QB", "qs")
+        mm(P(6, 1), "NI", "CO", True, False)
+        count(range(0, 8))
+        mms(P(4, 1), ("I", "KA"), ("NI", "DW"), ("TR", "DO"))
+        act("KA", P(4, 1), F_.Relu)
+        count(range(8, 16))
+        diag()
+        if last:
+            mms(P(4, 0), ("IR", "KA"))
+        ts("ll", X("b7", 0, 16), 2048.0, A_.add)
+        act("XH", IND(WD, X("ll")), F_.Copy)
+        tt("p2", "cmd", X("b6", 16, 32), A_.mult)
+        tt("R1B", "LO", P(1, 1), A_.mult)
+        if not last:
+            tt("EV", "DW", P(7, 1), A_.mult)
+        diag_add()
+        act("CW", P(6, 1), F_.Relu, -1.0)
+        mms(P(3, 0), ("HALF", "XG"), ("HALF", "XH"))
+        wrap(X("b6", 32, 48), "CW")
+        ts("qmd", "ql", 1.0, A_.mult)
+        tt("qmd", "qmd", "dumx", A_.subtract)
+        if last:
+            leave(rnd)
+        else:
+            mms(P(5, 1), ("I", "KA"), ("NSH", "KA"), ("B", "OA"), ("NI", "ONES"), ("BN4", "LO"), ("BN4", "CO"))
+            act("OA", P(5, 1), F_.Relu)
+        ts("XI", P(3, 0), -0.25, A_.add)
+        tt("px", "qmd", X("b6", 32, 48), A_.mult)
+        tt("yx2", "px", "dumx", A_.add)
+        cp("yxl", "yx2")
+        cp(IND(WDS, X("yxl")), "XI")
+        if fin:
+            cp(X("D", 4095, 4096), X("savd", 15, 16))
+            dma("y", "d6", T.yd[:], T.D[:, 0:4096], [("D", 0, 4096, 1)], [])
+        else:
+            for c in range(4):
+                gq(c, "LQ1" if last else lst)
+            wrap(X("b7", 16, 32), "LO")
+            tt("p1", "vmd", X("b7", 16, 32), A_.mult)
+        mms(P(5, 0), ("B", "R1A"), ("B", "R1B"))
+        mms(P(4, 0), ("B", "R2A"))
+        if not last:
+            tt("TP", "OA", P(1, 1), A_.mult)
+            mms(P(0, 1), ("B", "TP"))
+            mms(P(7, 0), ("I", "VB"), ("I", "EV"), ("BN1K", "OA"), ("K1", "ONES"))
+        ts("W1", P(5, 0), PM, A_.is_equal)
+        ts("W2", P(4, 0), PM, A_.is_equal)
+        mms(P(3, 1), ("I", "W2"), ("NI", "W1"), ("B", "CO"))
+        if not last:
+            ts("OT", P(0, 1), PM, A_.is_equal, 1.0 / 16, A_.mult)
+            cp("VB", P(7, 0))
+            lists()
+        tt("ye2", "p2", "dum", A_.add)
+        cp("yel", "ye2")
+        if not fin:
+            mms(P(4, 0), ("BP4K", "LO"), ("IN4K", "W1"))
+            mms(P(5, 0), ("I", "NA%d" % rnd), ("I2K", "W1"))
+            mms(P(7, 1), (X("IF"), "CC"), ("BP4K", "CO"), ("IN4K", "ONES"))
+            tt("VA", "CV", P(4, 0), A_.min)
+            tt("yc2", "ye2", "p1", A_.add)
+            cp("ycl", "yc2")
+            tt("VBB", "VA", P(5, 0), A_.max)
+        ts("W2G", P(3, 1), 1.5, A_.is_gt)
+        mms(P(0, 0), ("I", "LC"), ("TRP4K", "CO"))
+        if not fin:
+            mms(P(3, 0), ("I", "NB%d" % rnd), ("I2K", "W2G"))
+            cn = X("C", base, base + 512, 2)
+            tt(cn, cn, P(7, 1), A_.max)
+            tt("VC", "VBB", P(3, 0), A_.max)
+            cp(IND(WCS, X("ycl")), "VC")
+        mms(P(2, 0), ("I", "LC"), ("TRN4K", "CO"), ("K6", "ONES"))
+        mms(P(4, 1), ("I", qc), ("TRN4K", "LO"), ("K6", "ONES"))
+        mms(P(5, 1), ("I", qc), ("TRN4K", "CO"), ("BN4K", "W2G"), ("K10", "ONES"))
+        if last and not fin:
+            prep("LQ1", "QC1", "QH1")
+            roots("QC1", "QH1")
+            qres("QC1", "QH1")
+        ts("EC", P(0, 0), 2048.0, A_.add, 4095.0, A_.min)
+        cp(IND(WES, X("yel")), "EC")
+        ev, od = X("E", base, base + 512, 2), X("E", base + 1, base + 512, 2)
+        tt(ev, ev, P(2, 0), A_.min)
+        tt(od, od, P(5, 1), A_.min)
+        tt(ev, ev, P(4, 1), A_.min)
+
+    cp("QU", "qin")
+    prep("QU", "QC0", "QH0")
+    ts("dum", "dum", PM, A_.add)
+    roots("QC0", "QH0")
+    qres("QC0", "QH0")
+    cp(X("C", 0, 832), "cin")
+    cp(X("D", 4080, 4096), "savd")
+    fill(X("D", 4095, 4096), 20000.0)
+    for c in range(4):
+        gq(c, "QU")
+    for rnd in range(2):
+        lst, qc = ("QU", "LQ1")[rnd], "QC%d" % rnd
+        for s in range(3):
+            walk(rnd, s, lst, qc)
+            decide(rnd, s, lst, qc)
+    cp(X("E", 0, 1), X("save", 0, 1))
+    dma("y", "d7", T.ye[:], T.E[:, 0:1856], [("E", 0, 1856, 1)], [])
+    dma("y", "d5", T.yr[:, 64:256], T.YRL[:, 64:256], [("YRL", 64, 256, 1)], [])
+    finish("y")

@@ -6,7 +6,7 @@ F_ = ActivationFunctionType
 BF, HF, FF, II, UU = "bfloat16", "float16", "float32", "int32", "uint16"
 SCRATCH = {}
 MATS = ["B", "I", "TR", "U", "TS", "NI", "NB", "N16", "R0", "R016", "HALF", "BN4", "TRN4K", "TRP4K", "BN4K", "BP4K",
-        "IN4K", "I2K", "SH", "NSH", "IR", "K6", "K10", "K18", "BN1K", "K1", "K20"] + ["S%d" % f for f in range(16)]
+        "IN4K", "I2K", "SH", "ISH", "IR", "K6", "K10", "K18", "BN1K", "K20"] + ["S%d" % f for f in range(16)]
 
 
 def _decl():
@@ -18,13 +18,13 @@ def _decl():
     sb(832, II, "ein", "cin"), sb(256, II, "qin", "XI", "HP", "HH")
     sb(256, UU, "QU", "QN", "LQ1", "LU")
     sb(256, HF, "QC0", "QH0", "QC1", "QH1", "VB", "P16", "BAD", "NN", "CQ", "CL", "EV", "LC", "LH", "QB", "TP", "DG",
-       "R1A", "R1B", "R2A", "W1", "W2", "W2G", "OT", "NA0", "NB0", "NA1", "NB1", "DIAG")
-    sb(256, BF, "ONES", "OA", "KA", "GS", "ACT", "OCC", "CO", "DO", "LO", "FO", "DW", "XG", "XH", "CW")
-    sb(256, FF, "CV", "CC", "VA", "VBB", "VC", "EC", "QF", "HM", "HT", "HD", "HR", "HQ", "ST", "YRL", "YRO", "i256", "nb")
+       "R1A", "R1B", "R2A", "OT", "DIAG", "NA0", "NA1")
+    sb(256, BF, "ONES", "OA", "KA", "GS", "OCC", "AW", "AX", "W1", "W2", "W2G", "nb", "CO", "DO", "LO", "FO", "DW", "XG", "XH", "CW")
+    sb(256, FF, "CV", "CC", "VA", "NV", "EC", "QF", "HM", "HT", "HD", "HR", "HQ", "ST", "YRL", "YRO", "i256")
     sb(16, UU, "vl", "cu", "ql", "ll", "yel", "ycl", "yxl", "ysl")
-    sb(16, FF, "vs", "cf", "dum", "dumx", "vmd", "cmd", "p1", "p2", "ye2", "yc2", "qs", "x1", "qmd", "px", "yx2", "ps", "ys2")
-    sb(128, FF, "im", "ih", "il", "IF"), sb(128, BF, "sl"), sb(8, FF, "gi", "pf", "pm", "pv", "p0", "save"), sb(8, II, "pi", "pj", "pd")
-    sb(8, BF, "g8"), sb(16, BF, "savd")
+    sb(16, FF, "vs", "dum", "dumx", "vmd", "aw", "cmd", "p1", "p2", "ye2", "yc2", "qs", "x1", "qmd", "px", "yx2", "ps", "ys2")
+    sb(128, FF, "im", "ih", "il", "IF"), sb(128, BF, "sl"), sb(8, FF, "gi", "npm", "pf", "pm", "pv", "p0", "save")
+    sb(8, II, "pi", "pj", "pd"), sb(8, BF, "g8"), sb(16, BF, "savd")
     for b in range(8):
         SCRATCH["b%d" % b] = ("psum", [128, 512], FF)
 
@@ -151,7 +151,8 @@ def rank_program(g, core, T, topo):
 
     def act(out, a, f, scale=1.0, bias=0.0):
         out, a = O(out), O(a)
-        op("s", lambda e: e.activation(out[0], a[0], f, bias=bias, scale=scale), a[1], out[1])
+        b, r = (bias[0], bias[1]) if isinstance(bias, tuple) else (bias, [])
+        op("s", lambda e: e.activation(out[0], a[0], f, bias=b, scale=scale), a[1] + r, out[1])
 
     def iota(out, pat, base, cm):
         out = O(out)
@@ -191,9 +192,9 @@ def rank_program(g, core, T, topo):
     iota(X("C", 832, 2112), [[0, 1280]], 0, 0)
     iota("i256", [[0, 16], [1, 16]], 0, 0)
     iota(X("E", 832, 2112), [[0, 1280]], 4095, 0)
-    iota("nb", [[2, 256]], 832 - 2048, 0)
+    iota("nb", [[2, 256]], 0, 0)
     iota("OCT", [[0, 2112]], 0, 0)
-    PM, PV, PF, P0 = X("pm", 0, 1), X("pv", 0, 1), X("pf", 0, 1), X("p0", 0, 1)
+    NPM, PM, PV, PF, P0 = X("npm", 0, 1), X("pm", 0, 1), X("pv", 0, 1), X("pf", 0, 1), X("p0", 0, 1)
     fill("ONES", 1.0)
     s0 = 128 * MATS.index("S0")
     fill(X("cm", s0, s0 + 2048), 0.0)
@@ -203,6 +204,7 @@ def rank_program(g, core, T, topo):
     cp("pf", "pi")
     cp("pm", "pj")
     cp("pv", "pd")
+    ts("npm", "pj", -1.0, A_.mult)
     ts("p0", "pj", 0.0, A_.is_equal)
     ts(M("B"), "ih", PV, A_.is_equal)
     ts(M("I"), "im", PF, A_.is_equal)
@@ -217,8 +219,7 @@ def rank_program(g, core, T, topo):
             act(X("cm", s0 + 129 * f, s0 + 128 * f + 128, 16), "g8", F_.Copy)
     ts("sl", "il", PM, A_.is_ge)
     for nm, a, s in (("K20", "I", 1048576.0), ("HALF", "I", 0.5), ("BN4", "B", -4.0), ("BN4K", "B", -4096.0), ("BP4K", "B", 4096.0),
-                     ("IN4K", "I", -4096.0), ("I2K", "I", 2048.0), ("K6", "I", 6144.0), ("K10", "I", 10240.0), ("BN1K", "B", -1024.0),
-                     ("K1", "I", 1024.0)):
+                     ("IN4K", "I", -4096.0), ("I2K", "I", 2048.0), ("K6", "I", 6144.0), ("K10", "I", 10240.0), ("BN1K", "B", -1024.0)):
         act(M(nm), M(a), F_.Copy, s)
 
     def late_consts():
@@ -226,17 +227,17 @@ def rank_program(g, core, T, topo):
         ts("DIAG", "i256", PM, A_.is_equal)
         tt(M("TS"), M("TR"), M("I"), A_.subtract)
         tt(M("U"), M("TS"), M("I"), A_.subtract)
-        ts("dumx", "dum", 4112.0 - 1856.0, A_.add)
+        ts("dumx", "dum", 16.0, A_.mult, 4112.0 - 1856.0 - 2048.0, A_.add)
         ts("IF", "im", PF, A_.is_equal)
         ts(M("SH"), "im", PF, A_.subtract, 1.0, A_.is_equal)
         tt(M("SH"), M("SH"), M("B"), A_.mult)
         tt(M("IR"), M("I"), M("R0"), A_.mult)
         tt(M("IR"), M("I"), M("IR"), A_.subtract)
-        ts(M("NSH"), M("SH"), -1.0, A_.mult)
+        tt(M("ISH"), M("I"), M("SH"), A_.subtract)
+        ts("NA0", "nb", 832.0 - 2048.0, A_.add)
+        ts("NA1", "nb", 1344.0 - 2048.0, A_.add)
         ts(M("TRN4K"), M("TR"), -4096.0, A_.mult)
         ts(M("TRP4K"), M("TR"), 4096.0, A_.mult)
-        for j, nm in enumerate(("NA0", "NB0", "NA1", "NB1")):
-            ts(nm, "nb", float(j % 2 + 512 * (j // 2)), A_.add)
 
     WD, WDS = X("D", 0, 4112), X("D", 0, 4368)
     WC, WE, WCS, WES = X("C", 0, 1856), X("E", 0, 1856), X("C"), X("E")
@@ -275,25 +276,25 @@ def rank_program(g, core, T, topo):
     def gq(c, lst):
         act(X("XQ", 1024 * c, 1024 * c + 1024), IND(WD, X(lst, 64 * c, 64 * c + 64)), F_.Copy)
 
-    def gl(c):
-        act(X("XL", 1024 * (c - 2), 1024 * (c - 1)), IND(WD, X("LU", 64 * c, 64 * c + 64)), F_.Copy)
+    def gl(c, skip=0):
+        lo = 64 * c + skip
+        act(X("XL", 16 * lo - 2048, 1024 * (c - 1)), IND(WD, X("LU", lo, 64 * c + 64)), F_.Copy)
 
-    def diffs(c, banks):
-        for h, b in enumerate(banks):
-            lo = 1024 * c + 512 * h
-            mms(X("b%d" % b), ("I", X("XL", lo - 2048, lo - 1536)), ("NI", X("XQ", lo, lo + 512)))
+    def diffs(c, h, b):
+        lo = 1024 * c + 512 * h
+        mms(X("b%d" % b), ("I", X("XL", lo - 2048, lo - 1536)), ("NI", X("XQ", lo, lo + 512)))
 
-    def mags(c, banks):
-        for h, b in enumerate(banks):
-            lo = 1024 * c + 512 * h
-            act(X("DF", lo, lo + 512), X("b%d" % b), F_.Abs)
+    def mags(c, h, b):
+        lo = 1024 * c + 512 * h
+        act(X("DF", lo, lo + 512), X("b%d" % b), F_.Abs)
 
-    def sub(c):
-        sl = X("DF", 1024 * c, 1024 * c + 1024)
-        tt(sl, IND(WD, X("LU", 64 * c, 64 * c + 64)), X("XQ", 1024 * c, 1024 * c + 1024), A_.subtract)
+    def sub(c, j=0, n=1):
+        w = 64 // n
+        lo = 64 * c + w * j
+        tt(X("DF", 16 * lo, 16 * (lo + w)), IND(WD, X("LU", lo, lo + w)), X("XQ", 16 * lo, 16 * (lo + w)), A_.subtract)
 
-    def mag(c):
-        sl = X("DF", 1024 * c, 1024 * c + 1024)
+    def mag(c, w=64):
+        sl = X("DF", 1024 * c, 1024 * c + 16 * w)
         act(sl, sl, F_.Abs)
 
     def dist(c):
@@ -329,21 +330,19 @@ def rank_program(g, core, T, topo):
         cp("LU", IND(WE, X("cu")))
 
     def cmd():
-        ts("cf", "cu", 1.0, A_.mult)
-        tt("cmd", "cf", "dum", A_.subtract)
+        tt("cmd", W0, "dum", A_.subtract)
 
     def acts():
-        ts("ACT", P(6, 1), 0.0, A_.min, -1.0 / 16, A_.mult)
         cp("GS", P(6, 1))
-        wrap(X("b7", 0, 16), "ACT")
+        wrap(X("b7", 0, 16), "GS")
 
     def stamp(n):
         iota("ST", [[0, 256]], n, 0)
-        ts("vmd", "vs", 16.0, A_.mult)
-        tt("vmd", "vmd", "dum", A_.subtract)
-        tt("ps", "vmd", X("b7", 0, 16), A_.mult)
+        tt("vmd", "vs", "dum", A_.subtract)
+        ts("aw", X("b7", 0, 16), 0.0, A_.min, -1.0 / 16, A_.mult)
+        tt("ps", "vmd", "aw", A_.mult)
         tt("ys2", "ps", "dum", A_.add)
-        cp("ysl", "ys2")
+        ts("ysl", "ys2", 16.0, A_.mult)
         cp(IND(X("OCT"), X("ysl")), "ST")
 
     def gates(n):
@@ -386,7 +385,7 @@ def rank_program(g, core, T, topo):
         note("ar%d" % i, 4 * (NR - 1), [], [(dst, 64, 256, 1)], None)
 
     def leave(rnd):
-        tt("HR", P(4, 0), "HD", A_.mult)
+        tt("HR", P(5, 1), "HD", A_.mult)
         if rnd == 0:
             tt("HQ", "HR", P(7, 1), A_.add)
             cp("QN", "HQ")
@@ -401,7 +400,6 @@ def rank_program(g, core, T, topo):
         n, first = 3 * rnd + s + 1, rnd == 0 and s == 0
         child()
         causal(range(0, 8), "VB", "vs")
-        act("CV", IND(WC, X("vl")), F_.Copy)
         if first:
             late_consts()
             cp(X("E", 0, 832), "ein")
@@ -419,43 +417,58 @@ def rank_program(g, core, T, topo):
             lh()
             cmd()
             diag_add()
-            for c in range(4):
-                sub(c)
-                if c == 0:
-                    acts()
-                mag(c)
-                dist(c)
-                if c == 2:
-                    stamp(n)
-                    gates2()
-                    lres()
-            gates(n)
-        else:
-            gl(2)
-            sub(0)
             gl(3)
-            diffs(2, (4, 5))
-            causal(range(8, 16), "VB", "vs")
-            count(range(8, 16))
-            diag()
-            mags(2, (4, 5))
-            lh()
-            cmd()
-            diag_add()
-            sub(1)
-            diffs(3, (3, 5))
-            lres()
+            sub(0)
             acts()
             mag(0)
             dist(0)
-            mags(3, (3, 5))
+            sub(1)
+            diffs(3, 0, 4)
+            diffs(3, 1, 5)
+            mag(1)
+            dist(1)
+            stamp(n)
+            mags(3, 0, 4)
+            mags(3, 1, 5)
+            dist(3)
+            sub(2)
+            gates2()
+            lres()
+            mag(2)
             dist(2)
+        else:
+            gl(2, 32)
+            sub(0)
+            gl(3)
+            causal(range(8, 16), "VB", "vs")
+            diffs(2, 1, 4)
+            count(range(8, 16))
+            diag()
+            lh()
+            lres()
+            cmd()
+            mags(2, 1, 4)
+            sub(1, 0, 2)
+            diag_add()
+            sub(1, 1, 2)
+            diffs(3, 0, 5)
+            diffs(3, 1, 4)
+            acts()
+            mag(0)
+            dist(0)
+            mags(3, 0, 5)
+            mags(3, 1, 4)
+            sub(2, 0, 2)
+            dist(3)
             stamp(n)
             mag(1)
-            dist(3)
             gates2()
             dist(1)
-            gates(n)
+            mag(2, 32)
+            dist(2)
+        if s < 2 or rnd == 0:
+            act("CV", IND(WC, X("vl")), F_.Copy)
+        gates(n)
 
     def decide(rnd, s, lst, qc):
         base, last = 832 + 512 * rnd, s == 2
@@ -474,103 +487,122 @@ def rank_program(g, core, T, topo):
         mm(P(4, 0), "U", "BAD")
         mm(P(4, 0), "NI", "NN", False, True)
         act("DO", P(4, 0), F_.Relu, -1.0, -2.0)
+        if not fin:
+            act("CC", IND(WC, X("cu")), F_.Copy)
         mms(P(3, 1), ("B", "CQ"))
         wrap(W0, "CQ")
         wrap(X("b6", 16, 32), "CO")
         mms(P(0, 1), ("B", "FO"), ("I", "GS"))
         act("DW", P(0, 1), F_.Relu, -1.0)
-        if not fin:
-            act("CC", IND(WC, X("cu")), F_.Copy)
+        mms(P(5, 1), ("I", "LC"), ("TRP4K", "CO"))
+        act("EC", P(5, 1), F_.Relu, -1.0, 2047.0)
         tt("CL", "CO", P(2, 0), A_.mult)
         tt("R1A", "CO", P(2, 1), A_.mult)
-        tt("R2A", "CO", P(1, 1), A_.mult)
         cp("QB", P(3, 1))
+        tt("R2A", "CO", P(1, 1), A_.mult)
+        tt("R1B", "LO", P(1, 1), A_.mult)
         ts("x1", X("b6", 16, 32), -5000.0, A_.mult, 5000.0, A_.add)
         tt("qs", "x1", W0, A_.add)
         ts("ql", W0, 2048.0, A_.add)
-        act("XG", IND(WD, X("ql")), F_.Copy)
-        if last:
-            mms(P(7, 1), ("I", qc), ("I2K", "ONES"))
-        wrap(X("b7", 0, 16), "CL")
-        causal(range(0, 16), "QB", "qs")
-        mm(P(6, 1), "NI", "CO", True, False)
-        count(range(0, 8))
-        mms(P(4, 1), ("I", "KA"), ("NI", "DW"), ("TR", "DO"))
-        act("KA", P(4, 1), F_.Relu)
-        count(range(8, 16))
-        diag()
-        if last:
-            mms(P(4, 0), ("IR", "KA"))
-        ts("ll", X("b7", 0, 16), 2048.0, A_.add)
-        act("XH", IND(WD, X("ll")), F_.Copy)
+        tt("qmd", W0, "dumx", A_.subtract)
         tt("p2", "cmd", X("b6", 16, 32), A_.mult)
-        tt("R1B", "LO", P(1, 1), A_.mult)
+        act("XG", IND(WD, X("ql")), F_.Copy)
+        mms(P(0, 1), ("B", "R2A"))
+        mms(P(0, 0), ("B", "R1A"), ("B", "R1B"))
+        act("AX", P(0, 1), F_.Abs, 1.0, NPM)
+        act("AW", P(0, 0), F_.Abs, 1.0, NPM)
+        act("W2", "AX", F_.Relu, -1.0, 1.0)
+        act("W1", "AW", F_.Relu, -1.0, 1.0)
+        causal(range(0, 16), "QB", "qs")
         if not last:
             tt("EV", "DW", P(7, 1), A_.mult)
+        mm(P(6, 1), "NI", "CO", True, False)
+        count(range(0, 16))
+        diag()
+        wrap(X("b7", 0, 16), "CL")
         diag_add()
+        ts("ll", X("b7", 0, 16), 2048.0, A_.add)
         act("CW", P(6, 1), F_.Relu, -1.0)
-        mms(P(3, 0), ("HALF", "XG"), ("HALF", "XH"))
+        mms(P(4, 1), ("I", "KA"), ("NI", "DW"), ("TR", "DO"))
+        act("KA", P(4, 1), F_.Relu)
+        act("XH", IND(WD, X("ll")), F_.Copy)
+        mms(P(0, 1), ("I", "W2"), ("NI", "W1"), ("B", "CO"))
         wrap(X("b6", 32, 48), "CW")
-        ts("qmd", "ql", 1.0, A_.mult)
-        tt("qmd", "qmd", "dumx", A_.subtract)
+        mms(P(3, 1), ("HALF", "XG"), ("HALF", "XH"))
+        act("W2G", P(0, 1), F_.Relu, 1.0, -1.0)
+        tt("ye2", "p2", "dum", A_.add)
+        ts("yel", "ye2", 16.0, A_.mult)
+        if fin:
+            ts("XI", P(3, 1), -0.25, A_.add)
         if last:
+            mms(P(5, 1), ("IR", "KA"))
+            mms(P(7, 1), ("I", qc), ("I2K", "ONES"))
             leave(rnd)
         else:
-            mms(P(5, 1), ("I", "KA"), ("NSH", "KA"), ("B", "OA"), ("NI", "ONES"), ("BN4", "LO"), ("BN4", "CO"))
-            act("OA", P(5, 1), F_.Relu)
-        ts("XI", P(3, 0), -0.25, A_.add)
+            mms(P(5, 1), ("B", "OA"), ("BN4", "LO"), ("BN4", "CO"), ("ISH", "KA"))
+            act("OA", P(5, 1), F_.Relu, 1.0, -1.0)
+        if fin:
+            edges_out(base, qc)
+            cp(X("E", 0, 1), X("save", 0, 1))
+            dma("y", "d7", T.ye[:], T.E[:, 0:1856], [("E", 0, 1856, 1)], [])
         tt("px", "qmd", X("b6", 32, 48), A_.mult)
         tt("yx2", "px", "dumx", A_.add)
-        cp("yxl", "yx2")
+        if not fin:
+            ts("XI", P(3, 1), -0.25, A_.add)
+        ts("yxl", "yx2", 2048.0, A_.add)
         cp(IND(WDS, X("yxl")), "XI")
         if fin:
             cp(X("D", 4095, 4096), X("savd", 15, 16))
             dma("y", "d6", T.yd[:], T.D[:, 0:4096], [("D", 0, 4096, 1)], [])
-        else:
-            for c in range(4):
-                gq(c, "LQ1" if last else lst)
-            wrap(X("b7", 16, 32), "LO")
-            tt("p1", "vmd", X("b7", 16, 32), A_.mult)
-        mms(P(5, 0), ("B", "R1A"), ("B", "R1B"))
-        mms(P(4, 0), ("B", "R2A"))
+            return
+        wl = X("b6", 48, 64)
+        wrap(wl, "LO")
+        mms(P(0, 0), (X("IF"), "CV"), ("BP4K", "LO"), ("IN4K", "W1"))
+        act("VA", P(0, 0), F_.Relu, 1.0, -4096.0)
+        gq(0, "LQ1" if last else lst)
+        mms(P(2, 0), ("I", "LC"), ("TRN4K", "CO"), ("K6", "ONES"))
+        mms(P(4, 0), ("I", "NA%d" % rnd), ("I2K", "W1"), ("I2K", "W2G"), ("I", "W2G"))
+        act("NV", P(4, 0), F_.Copy)
+        for c in range(1, 4):
+            gq(c, "LQ1" if last else lst)
+        tt("p1", "vmd", wl, A_.mult)
         if not last:
             tt("TP", "OA", P(1, 1), A_.mult)
+            mms(P(7, 0), ("I", "VB"), ("I", "EV"), ("BN1K", "OA"))
             mms(P(0, 1), ("B", "TP"))
-            mms(P(7, 0), ("I", "VB"), ("I", "EV"), ("BN1K", "OA"), ("K1", "ONES"))
-        ts("W1", P(5, 0), PM, A_.is_equal)
-        ts("W2", P(4, 0), PM, A_.is_equal)
-        mms(P(3, 1), ("I", "W2"), ("NI", "W1"), ("B", "CO"))
+        tt("yc2", "ye2", "p1", A_.add)
+        ts(IND(WES, X("yel")), "EC", -1.0, A_.mult, 4095.0, A_.add)
+        ts("ycl", "yc2", 16.0, A_.mult)
+        if not last:
+            ts("VB", P(7, 0), 1024.0, A_.add)
+        mms(P(5, 1), ("I", qc), ("TRN4K", "CO"), ("BN4K", "W2G"), ("K10", "ONES"))
+        if not last:
+            wrap(W0, "VB")
+        mms(P(4, 1), ("I", qc), ("TRN4K", "LO"), ("K6", "ONES"))
         if not last:
             ts("OT", P(0, 1), PM, A_.is_equal, 1.0 / 16, A_.mult)
-            cp("VB", P(7, 0))
-            lists()
-        tt("ye2", "p2", "dum", A_.add)
-        cp("yel", "ye2")
-        if not fin:
-            mms(P(4, 0), ("BP4K", "LO"), ("IN4K", "W1"))
-            mms(P(5, 0), ("I", "NA%d" % rnd), ("I2K", "W1"))
-            mms(P(7, 1), (X("IF"), "CC"), ("BP4K", "CO"), ("IN4K", "ONES"))
-            tt("VA", "CV", P(4, 0), A_.min)
-            tt("yc2", "ye2", "p1", A_.add)
-            cp("ycl", "yc2")
-            tt("VBB", "VA", P(5, 0), A_.max)
-        ts("W2G", P(3, 1), 1.5, A_.is_gt)
-        mms(P(0, 0), ("I", "LC"), ("TRP4K", "CO"))
-        if not fin:
-            mms(P(3, 0), ("I", "NB%d" % rnd), ("I2K", "W2G"))
-            cn = X("C", base, base + 512, 2)
-            tt(cn, cn, P(7, 1), A_.max)
-            tt("VC", "VBB", P(3, 0), A_.max)
-            cp(IND(WCS, X("ycl")), "VC")
+        else:
+            prep("LQ1", "QC1", "QH1")
+        ev, od = X("E", base, base + 512, 2), X("E", base + 1, base + 512, 2)
+        tt(ev, ev, P(2, 0), A_.min)
+        mms(P(7, 1), (X("IF"), "CC"), ("BP4K", "CO"), ("IN4K", "ONES"))
+        tt(IND(WCS, X("ycl")), "VA", "NV", A_.max)
+        tt(od, od, P(5, 1), A_.min)
+        if not last:
+            ts("vl", W0, 1855.0, A_.min)
+            ts("vs", W0, 1.0 / 16, A_.mult)
+        tt(ev, ev, P(4, 1), A_.min)
+        cn = X("C", base, base + 512, 2)
+        tt(cn, cn, P(7, 1), A_.max)
+        if last:
+            roots("QC1", "QH1")
+            qres("QC1", "QH1")
+
+    def edges_out(base, qc):
         mms(P(2, 0), ("I", "LC"), ("TRN4K", "CO"), ("K6", "ONES"))
         mms(P(4, 1), ("I", qc), ("TRN4K", "LO"), ("K6", "ONES"))
         mms(P(5, 1), ("I", qc), ("TRN4K", "CO"), ("BN4K", "W2G"), ("K10", "ONES"))
-        if last and not fin:
-            prep("LQ1", "QC1", "QH1")
-            roots("QC1", "QH1")
-            qres("QC1", "QH1")
-        ts("EC", P(0, 0), 2048.0, A_.add, 4095.0, A_.min)
-        cp(IND(WES, X("yel")), "EC")
+        ts(IND(WES, X("yel")), "EC", -1.0, A_.mult, 4095.0, A_.add)
         ev, od = X("E", base, base + 512, 2), X("E", base + 1, base + 512, 2)
         tt(ev, ev, P(2, 0), A_.min)
         tt(od, od, P(5, 1), A_.min)
@@ -579,6 +611,7 @@ def rank_program(g, core, T, topo):
     cp("QU", "qin")
     prep("QU", "QC0", "QH0")
     ts("dum", "dum", PM, A_.add)
+    ts("dum", "dum", 1.0 / 16, A_.mult)
     roots("QC0", "QH0")
     qres("QC0", "QH0")
     cp(X("C", 0, 832), "cin")
@@ -591,7 +624,5 @@ def rank_program(g, core, T, topo):
         for s in range(3):
             walk(rnd, s, lst, qc)
             decide(rnd, s, lst, qc)
-    cp(X("E", 0, 1), X("save", 0, 1))
-    dma("y", "d7", T.ye[:], T.E[:, 0:1856], [("E", 0, 1856, 1)], [])
     dma("y", "d5", T.yr[:, 64:256], T.YRL[:, 64:256], [("YRL", 64, 256, 1)], [])
     finish("y")

from concourse.bass import DstId, RemoteDMATransfer
from concourse.mybir import AluOpType, ActivationFunctionType

A_ = AluOpType
F_ = ActivationFunctionType
BF, HF, FF, II, UU = "bfloat16", "float16", "float32", "int32", "uint16"
SCRATCH = {}
MATS = ["B", "I", "TR", "U", "TS", "NI", "NB", "N16", "R0", "R016", "HALF", "BN4", "TRN4K", "TRP4K", "BN4K", "BP4K",
        "IN4K", "I2K", "SH", "ISH", "IR", "K6", "K10", "K18", "BN1K", "K20"] + ["S%d" % f for f in range(16)]


def _decl():
    def sb(w, d, *names):
        for n in names:
            SCRATCH[n] = ("sbuf", [128, w], d)
    sb(4368, BF, "D"), sb(2112, FF, "E", "C", "OCT"), sb(4096, BF, "XQ", "DF"), sb(2048, BF, "XL"), sb(4096, HF, "EQA")
    sb(128 * len(MATS), BF, "cm")
    sb(832, II, "ein", "cin"), sb(256, II, "qin", "XI", "HP", "HH")
    sb(256, UU, "QU", "QN", "LQ1", "LU")
    sb(256, HF, "QC0", "QH0", "QC1", "QH1", "VB", "P16", "BAD", "NN", "CQ", "CL", "EV", "LC", "LH", "QB", "TP", "DG",
       "R1A", "R1B", "R2A", "OT", "DIAG", "NA0", "NA1")
    sb(256, BF, "ONES", "OA", "KA", "GS", "OCC", "AW", "AX", "W1", "W2", "W2G", "nb", "CO", "DO", "LO", "FO", "DW", "XG", "XH", "CW")
    sb(256, FF, "CV", "CC", "VA", "NV", "EC", "QF", "HM", "HT", "HD", "HR", "HQ", "ST", "YRL", "YRO", "i256")
    sb(16, UU, "vl", "cu", "ql", "ll", "yel", "ycl", "yxl", "ysl")
    sb(16, FF, "vs", "dum", "dumx", "vmd", "aw", "cmd", "p1", "p2", "ye2", "yc2", "qs", "x1", "qmd", "px", "yx2", "ps", "ys2")
    sb(128, FF, "im", "ih", "il", "IF"), sb(128, BF, "sl"), sb(8, FF, "gi", "npm", "pf", "pm", "pv", "p0", "save")
    sb(8, II, "pi", "pj", "pd"), sb(8, BF, "g8"), sb(16, BF, "savd")
    for b in range(8):
        SCRATCH["b%d" % b] = ("psum", [128, 512], FF)


_decl()
SEMAPHORES = ["qv", "qs", "qt", "qg"] + ["d%d" % i for i in range(9)] + ["ls0", "ls1", "ar0", "ar1"]


def tracker(g, T):
    eng = {"v": g.vector, "s": g.scalar, "t": g.tensor, "g": g, "y": g.sync}
    obs = {q: {} for q in eng}
    cnt, snap, acc, bank, tot = {}, {}, {}, {}, {}

    def sem(pq):
        return T.sem["q" + pq] if pq in eng else T.sem[pq]

    def clash(a, b):
        if a[1] <= b[0] or b[1] <= a[0]:
            return False
        return not (a[2] == b[2] > 1 and (a[0] - b[0]) % a[2])

    def learn(q, pq, n):
        o = obs[q]
        if o.get(pq, 0) >= n:
            return
        o[pq] = n
        for k, m in snap.get((pq, n), {}).items():
            if o.get(k, 0) < m:
                o[k] = m

    def waits(q, reads, writes):
        req = {}
        for w, regs in ((0, reads), (1, writes)):
            for nm, lo, hi, st in regs:
                if SCRATCH[nm][0] == "psum":
                    for pq, n in bank.get(nm, {}).items():
                        if pq != q:
                            req[pq] = max(req.get(pq, 0), n)
                    continue
                for r, pq, n, pw in acc.get(nm, []):
                    if not (w or pw) or not clash(r, (lo, hi, st)):
                        continue
                    req[pq] = max(req.get(pq, 0), n)
        for pq in sorted(req, key=lambda k: -req[k]):
            if obs[q].get(pq, 0) < req[pq]:
                eng[q].wait_ge(sem(pq), req[pq])
                learn(q, pq, req[pq])

    def note(pq, n, reads, writes, issuer):
        snap[(pq, n)] = dict(obs[issuer]) if issuer else {}
        for w, regs in ((0, reads), (1, writes)):
            for nm, lo, hi, st in regs:
                if SCRATCH[nm][0] == "psum":
                    bank[nm] = {pq: n}
                    continue
                keep = []
                for e in acc.get(nm, []):
                    r = e[0]
                    inside = lo <= r[0] and r[1] <= hi and (st == 1 or r == (lo, hi, st))
                    if not (inside and (w or (e[1] == pq and not e[3]))):
                        keep.append(e)
                acc[nm] = keep + [((lo, hi, st), pq, n, w)]

    def op(q, fn, reads, writes):
        waits(q, reads, writes)
        n = cnt.get(q, 0) + 1
        cnt[q] = tot[q] = n
        fn(eng[q]).then_inc(sem(q), 1)
        note(q, n, reads, writes, q)

    def dma(q, name, out, in_, reads, writes):
        waits(q, reads, writes)
        eng[q].dma_start(out, in_).then_inc(T.sem[name], 16)
        tot[name] = 16
        note(name, 16, reads, writes, q)

    def finish(q):
        for pq, n in tot.items():
            if obs[q].get(pq, 0) < n:
                eng[q].wait_ge(sem(pq), n)
                learn(q, pq, n)
    return op, dma, waits, note, tot, finish


def rank_program(g, core, T, topo):
    rank = T.rank_of(core)
    if rank is None:
        return
    NR = len(T.cores)
    op, dma, waits, note, tot, finish = tracker(g, T)

    def X(nm, lo=0, hi=None, st=1):
        hi = SCRATCH[nm][1][1] if hi is None else hi
        return (T[nm][:, lo:hi:st] if st > 1 else T[nm][:, lo:hi], [(nm, lo, hi, st)])

    def IND(win, off):
        return (win[0].indirect(off[0]), win[1] + off[1])

    def O(x):
        return X(x) if isinstance(x, str) else x

    def tt(out, a, b, f):
        out, a, b = O(out), O(a), O(b)
        op("v", lambda e: e.tensor_tensor(out[0], a[0], b[0], f), a[1] + b[1], out[1])

    def ts(out, a, s1, f1, s2=None, f2=None):
        out, a = O(out), O(a)
        r, v1 = list(a[1]), s1
        if isinstance(s1, tuple):
            v1 = s1[0]
            r = r + s1[1]
        if f2 is None:
            op("v", lambda e: e.tensor_scalar(out[0], a[0], v1, None, f1), r, out[1])
        else:
            op("v", lambda e: e.tensor_scalar(out[0], a[0], v1, s2, f1, f2), r, out[1])

    def cp(out, a):
        out, a = O(out), O(a)
        op("v", lambda e: e.tensor_copy(out[0], a[0]), a[1], out[1])

    def fill(out, c):
        out = O(out)
        op("v", lambda e: e.memset(out[0], c), [], out[1])

    def act(out, a, f, scale=1.0, bias=0.0):
        out, a = O(out), O(a)
        b, r = (bias[0], bias[1]) if isinstance(bias, tuple) else (bias, [])
        op("s", lambda e: e.activation(out[0], a[0], f, bias=b, scale=scale), a[1] + r, out[1])

    def iota(out, pat, base, cm):
        out = O(out)
        op("g", lambda e: e.iota(out[0], pat, base, cm, allow_small_or_imprecise_dtypes=True), [], out[1])

    def M(nm):
        j = MATS.index(nm)
        return X("cm", 128 * j, 128 * j + 128)

    def mm(out, m, rhs, start=False, stop=False):
        m, rhs = (M(m) if isinstance(m, str) else m), O(rhs)
        op("t", lambda e: e.matmul(out[0], m[0], rhs[0], start, stop), m[1] + rhs[1], out[1])

    def mms(out, *pairs):
        for j, (m, rhs) in enumerate(pairs):
            mm(out, m, rhs, j == 0, j == len(pairs) - 1)

    def wrap(out, src):
        for f in range(16):
            mm(out, "S%d" % f, X(src, f, 256, 16), f == 0, f == 15)

    def P(b, h):
        return X("b%d" % b, 256 * h, 256 * h + 256)

    dma("y", "d0", T.qin[:], T.req[:], [], [("qin", 0, 256, 1)])
    dma("s", "d1", T.cin[:], T.child[:], [], [("cin", 0, 832, 1)])
    dma("y", "d8", T.savd[:], T.desc[:, 4080:4096], [], [("savd", 0, 16, 1)])
    dma("y", "d2", T.D[:, 0:4080], T.desc[:, 0:4080], [], [("D", 0, 4080, 1)])
    dma("s", "d3", T.ein[:], T.edge[:], [], [("ein", 0, 832, 1)])

    iota("pi", [[0, 8]], 0, 1)
    iota("ih", [[1, 8], [0, 16]], 0, 0)
    iota("im", [[1, 128]], 0, 0)
    iota("gi", [[1, 8]], 0, 0)
    iota("il", [[0, 8], [1, 16]], 0, 0)
    iota("dum", [[16, 16]], 1856, 0)
    iota(X("C", 832, 2112), [[0, 1280]], 0, 0)
    iota("i256", [[0, 16], [1, 16]], 0, 0)
    iota(X("E", 832, 2112), [[0, 1280]], 4095, 0)
    iota("nb", [[2, 256]], 0, 0)
    iota("OCT", [[0, 2112]], 0, 0)
    NPM, PM, PV, PF, P0 = X("npm", 0, 1), X("pm", 0, 1), X("pv", 0, 1), X("pf", 0, 1), X("p0", 0, 1)
    fill("ONES", 1.0)
    s0 = 128 * MATS.index("S0")
    fill(X("cm", s0, s0 + 2048), 0.0)
    fill(X("D", 4096, 4368), 1000.0)
    ts("pj", "pi", 15, A_.bitwise_and)
    ts("pd", "pi", 4, A_.logical_shift_right)
    cp("pf", "pi")
    cp("pm", "pj")
    cp("pv", "pd")
    ts("npm", "pj", -1.0, A_.mult)
    ts("p0", "pj", 0.0, A_.is_equal)
    ts(M("B"), "ih", PV, A_.is_equal)
    ts(M("I"), "im", PF, A_.is_equal)
    ts("g8", "gi", PV, A_.is_equal)
    ts(M("R0"), M("B"), P0, A_.mult)
    for nm, a, s in (("R016", "R0", -16.0), ("K18", "I", 20480.0), ("N16", "I", -16.0), ("NI", "I", -1.0), ("NB", "B", -1.0)):
        act(M(nm), M(a), F_.Copy, s)
    for f in range(16):
        if f % 2:
            cp(X("cm", s0 + 129 * f, s0 + 128 * f + 128, 16), "g8")
        else:
            act(X("cm", s0 + 129 * f, s0 + 128 * f + 128, 16), "g8", F_.Copy)
    ts("sl", "il", PM, A_.is_ge)
    for nm, a, s in (("K20", "I", 1048576.0), ("HALF", "I", 0.5), ("BN4", "B", -4.0), ("BN4K", "B", -4096.0), ("BP4K", "B", 4096.0),
                     ("IN4K", "I", -4096.0), ("I2K", "I", 2048.0), ("K6", "I", 6144.0), ("K10", "I", 10240.0), ("BN1K", "B", -1024.0)):
        act(M(nm), M(a), F_.Copy, s)

    def late_consts():
        tt(M("TR"), "sl", M("B"), A_.mult)
        ts("DIAG", "i256", PM, A_.is_equal)
        tt(M("TS"), M("TR"), M("I"), A_.subtract)
        tt(M("U"), M("TS"), M("I"), A_.subtract)
        ts("dumx", "dum", 16.0, A_.mult, 4112.0 - 1856.0 - 2048.0, A_.add)
        ts("IF", "im", PF, A_.is_equal)
        ts(M("SH"), "im", PF, A_.subtract, 1.0, A_.is_equal)
        tt(M("SH"), M("SH"), M("B"), A_.mult)
        tt(M("IR"), M("I"), M("R0"), A_.mult)
        tt(M("IR"), M("I"), M("IR"), A_.subtract)
        tt(M("ISH"), M("I"), M("SH"), A_.subtract)
        ts("NA0", "nb", 832.0 - 2048.0, A_.add)
        ts("NA1", "nb", 1344.0 - 2048.0, A_.add)
        ts(M("TRN4K"), M("TR"), -4096.0, A_.mult)
        ts(M("TRP4K"), M("TR"), 4096.0, A_.mult)

    WD, WDS = X("D", 0, 4112), X("D", 0, 4368)
    WC, WE, WCS, WES = X("C", 0, 1856), X("E", 0, 1856), X("C"), X("E")
    W0 = X("b6", 0, 16)

    def prep(src, qc, qh):
        ts(qc, src, -2048.0, A_.add)
        ts(qh, src, 1.0 / 16, A_.mult, 1152 - 0.46875, A_.add)

    def lists():
        wrap(W0, "VB")
        ts("vl", W0, 1855.0, A_.min)
        ts("vs", W0, 1.0 / 16, A_.mult)

    def roots(qc, qh):
        mms(P(7, 0), ("R0", qh))
        mms(P(7, 1), ("R0", qc), ("R016", qh), ("K18", "ONES"))
        ts("VB", P(7, 0), -1152.0, A_.add, 1.0 / 16, A_.mult)
        ts("OT", P(7, 1), PM, A_.is_equal, 1.0 / 16, A_.mult)
        lists()
        ts("OA", "ONES", P0, A_.mult)
        fill("KA", 1.0)

    def qres(qc, qh):
        mms(P(1, 0), ("I", qc))
        mms(P(1, 1), ("I", qc), ("N16", qh), ("K18", "ONES"))

    def lh():
        ts("LC", "LU", -2048.0, A_.add)
        ts("LH", "LU", 1.0 / 16, A_.mult, 1152 - 0.46875, A_.add)

    def lres():
        mms(P(2, 0), ("I", "LC"))
        mms(P(2, 1), ("I", "LC"), ("N16", "LH"), ("K18", "ONES"))

    def gq(c, lst):
        act(X("XQ", 1024 * c, 1024 * c + 1024), IND(WD, X(lst, 64 * c, 64 * c + 64)), F_.Copy)

    def gl(c, skip=0):
        lo = 64 * c + skip
        act(X("XL", 16 * lo - 2048, 1024 * (c - 1)), IND(WD, X("LU", lo, 64 * c + 64)), F_.Copy)

    def diffs(c, h, b):
        lo = 1024 * c + 512 * h
        mms(X("b%d" % b), ("I", X("XL", lo - 2048, lo - 1536)), ("NI", X("XQ", lo, lo + 512)))

    def mags(c, h, b):
        lo = 1024 * c + 512 * h
        act(X("DF", lo, lo + 512), X("b%d" % b), F_.Abs)

    def sub(c, j=0, n=1):
        w = 64 // n
        lo = 64 * c + w * j
        tt(X("DF", 16 * lo, 16 * (lo + w)), IND(WD, X("LU", lo, lo + w)), X("XQ", 16 * lo, 16 * (lo + w)), A_.subtract)

    def mag(c, w=64):
        sl = X("DF", 1024 * c, 1024 * c + 16 * w)
        act(sl, sl, F_.Abs)

    def dist(c):
        o = X("b0", 64 * c, 64 * c + 64)
        mm(o, "K20", X("KA", 64 * c, 64 * c + 64), True, False)
        for k in range(16):
            mm(o, "S%d" % k, X("DF", 1024 * c + k, 1024 * c + 1024, 16), False, k == 15)

    def causal(cols, code, scal):
        for c in cols:
            ts(X("EQA", 256 * c, 512 * c + 256 - 272 * c), X(code, 16 * c, 256), X(scal, c, c + 1), A_.is_equal)

    def count(cols):
        for c in cols:
            if c < 15:
                mm(X("b6", 256 + 16 * (c + 1), 512), "B", X("EQA", 256 * c + 16, 512 * c + 256 - 272 * c))

    def diag():
        for c in range(16):
            mm(X("b3", 16 * c, 16 * c + 16), "TS", X("EQA", 256 * c, 256 * c + 16), True, True)

    def diag_add():
        tt("DG", P(3, 0), "DIAG", A_.mult)
        mm(P(6, 1), "B", "DG", False, True)

    def child():
        tt("P16", IND(WC, X("vl")), "OT", A_.mult)
        wrap(W0, "P16")
        mms(P(7, 1), ("B", "P16"), ("NI", "VB"))

    def edge():
        ts("cu", W0, 16.0, A_.mult)
        cp("LU", IND(WE, X("cu")))

    def cmd():
        tt("cmd", W0, "dum", A_.subtract)

    def acts():
        cp("GS", P(6, 1))
        wrap(X("b7", 0, 16), "GS")

    def stamp(n):
        iota("ST", [[0, 256]], n, 0)
        tt("vmd", "vs", "dum", A_.subtract)
        ts("aw", X("b7", 0, 16), 0.0, A_.min, -1.0 / 16, A_.mult)
        tt("ps", "vmd", "aw", A_.mult)
        tt("ys2", "ps", "dum", A_.add)
        ts("ysl", "ys2", 16.0, A_.mult)
        cp(IND(X("OCT"), X("ysl")), "ST")

    def gates(n):
        ts("OCC", IND(X("OCT", 0, 1856), X("cu")), float(n), A_.is_ge)
        mm(P(3, 0), "I", "OCC")

    def gates2():
        mm(P(3, 0), "I", "GS", True, False)
        mm(P(3, 0), "NI", "KA")
        mm(P(3, 0), "I", "OA")
        mm(P(5, 0), "I", "GS", True, False)
        mm(P(5, 0), "NI", "OA")
        mm(P(4, 0), "I", "GS", True, False)

    def hash_prep(lst, qc):
        cp("QF", lst)
        mms(P(0, 1), ("SH", qc), ("I2K", "ONES"))
        tt("HP", "QF", P(0, 1), A_.mult)
        ts("HH", "HP", 5, A_.logical_shift_right, 4095, A_.bitwise_and)
        ts("HM", "HH", 4095.0, A_.is_equal, -4095.0, A_.mult)
        tt("HT", "HH", "HM", A_.add)
        tt("HD", "HT", "QF", A_.subtract)

    def send(i, src, dst):
        used, tr, nls = set(), [], 0
        peers = [(e, T.cores[(rank + e) % NR]) for e in range(1, NR)]
        for e, c in sorted(peers, key=lambda x: len(topo.engines(core, x[1]))):
            es = [k for k in topo.engines(core, c) if k not in used][:4]
            used.update(es)
            nls += len(es)
            rid, pid = topo.addr(c)[0], topo.addr(c)[1]
            tr.append(RemoteDMATransfer(dst_ids=[DstId(rid=rid, pnc=pid)], dma_engine_mask=sum(1 << k for k in es), remote_sem=T.sem["ar%d" % i],
                                        src=T[src][:, 64 * e:64 * e + 64], dst=T[dst][:, 64 * e:64 * e + 64]))
        reg = [(src, 64, 256, 1)]
        waits("g", reg, [])
        g.remote_dma_fused(tr, local_sem=T.sem["ls%d" % i])
        tot["ls%d" % i] = nls
        note("ls%d" % i, nls, reg, [], "g")
        tot["ar%d" % i] = 4 * (NR - 1)
        note("ar%d" % i, 4 * (NR - 1), [], [(dst, 64, 256, 1)], None)

    def leave(rnd):
        tt("HR", P(5, 1), "HD", A_.mult)
        if rnd == 0:
            tt("HQ", "HR", P(7, 1), A_.add)
            cp("QN", "HQ")
            send(0, "QN", "LQ1")
            cp(X("LQ1", 0, 64), X("QN", 0, 64))
        else:
            tt("YRO", "HR", P(7, 1), A_.add)
            send(1, "YRO", "YRL")
            dma("y", "d4", T.yr[:, 0:64], T.YRO[:, 0:64], [("YRO", 0, 64, 1)], [])

    def walk(rnd, s, lst, qc):
        n, first = 3 * rnd + s + 1, rnd == 0 and s == 0
        child()
        causal(range(0, 8), "VB", "vs")
        if first:
            late_consts()
            cp(X("E", 0, 832), "ein")
            cp("save", X("E", 0, 8))
            fill(X("E", 0, 1), 4096.0)
        edge()
        mm(P(6, 1), "NB", "OA", True, False)
        count(range(0, 8))
        if s == 0:
            hash_prep(lst, qc)
        if first:
            causal(range(8, 16), "VB", "vs")
            count(range(8, 16))
            diag()
            lh()
            cmd()
            diag_add()
            gl(3)
            sub(0)
            acts()
            mag(0)
            dist(0)
            sub(1)
            diffs(3, 0, 4)
            diffs(3, 1, 5)
            mag(1)
            dist(1)
            stamp(n)
            mags(3, 0, 4)
            mags(3, 1, 5)
            dist(3)
            sub(2)
            gates2()
            lres()
            mag(2)
            dist(2)
        else:
            gl(2, 32)
            sub(0)
            gl(3)
            causal(range(8, 16), "VB", "vs")
            diffs(2, 1, 4)
            count(range(8, 16))
            diag()
            lh()
            lres()
            cmd()
            mags(2, 1, 4)
            sub(1, 0, 2)
            diag_add()
            sub(1, 1, 2)
            diffs(3, 0, 5)
            diffs(3, 1, 4)
            acts()
            mag(0)
            dist(0)
            mags(3, 0, 5)
            mags(3, 1, 4)
            sub(2, 0, 2)
            dist(3)
            stamp(n)
            mag(1)
            gates2()
            dist(1)
            mag(2, 32)
            dist(2)
        if s < 2 or rnd == 0:
            act("CV", IND(WC, X("vl")), F_.Copy)
        gates(n)

    def decide(rnd, s, lst, qc):
        base, last = 832 + 512 * rnd, s == 2
        fin = last and rnd == 1
        ts("BAD", P(0, 0), 1048576.0 + 700.5, A_.is_gt)
        ts("NN", P(0, 0), 1048576.0 + 200000.0, A_.is_gt)
        mm(P(3, 0), "U", "BAD")
        mm(P(3, 0), "I", "NN", False, True)
        act("CO", P(3, 0), F_.Relu, -1.0, -2.0)
        mms(P(0, 1), ("U", "BAD"), ("I", "NN"))
        act("FO", P(0, 1), F_.Relu, -1.0)
        tt("CQ", "CO", P(1, 0), A_.mult)
        mm(P(5, 0), "NI", "BAD")
        mm(P(5, 0), "I", "NN", False, True)
        act("LO", P(5, 0), F_.Relu, -1.0, -2.0)
        mm(P(4, 0), "U", "BAD")
        mm(P(4, 0), "NI", "NN", False, True)
        act("DO", P(4, 0), F_.Relu, -1.0, -2.0)
        if not fin:
            act("CC", IND(WC, X("cu")), F_.Copy)
        mms(P(3, 1), ("B", "CQ"))
        wrap(W0, "CQ")
        wrap(X("b6", 16, 32), "CO")
        mms(P(0, 1), ("B", "FO"), ("I", "GS"))
        act("DW", P(0, 1), F_.Relu, -1.0)
        mms(P(5, 1), ("I", "LC"), ("TRP4K", "CO"))
        act("EC", P(5, 1), F_.Relu, -1.0, 2047.0)
        tt("CL", "CO", P(2, 0), A_.mult)
        tt("R1A", "CO", P(2, 1), A_.mult)
        cp("QB", P(3, 1))
        tt("R2A", "CO", P(1, 1), A_.mult)
        tt("R1B", "LO", P(1, 1), A_.mult)
        ts("x1", X("b6", 16, 32), -5000.0, A_.mult, 5000.0, A_.add)
        tt("qs", "x1", W0, A_.add)
        ts("ql", W0, 2048.0, A_.add)
        tt("qmd", W0, "dumx", A_.subtract)
        tt("p2", "cmd", X("b6", 16, 32), A_.mult)
        act("XG", IND(WD, X("ql")), F_.Copy)
        mms(P(0, 1), ("B", "R2A"))
        mms(P(0, 0), ("B", "R1A"), ("B", "R1B"))
        act("AX", P(0, 1), F_.Abs, 1.0, NPM)
        act("AW", P(0, 0), F_.Abs, 1.0, NPM)
        act("W2", "AX", F_.Relu, -1.0, 1.0)
        act("W1", "AW", F_.Relu, -1.0, 1.0)
        causal(range(0, 16), "QB", "qs")
        if not last:
            tt("EV", "DW", P(7, 1), A_.mult)
        mm(P(6, 1), "NI", "CO", True, False)
        count(range(0, 16))
        diag()
        wrap(X("b7", 0, 16), "CL")
        diag_add()
        ts("ll", X("b7", 0, 16), 2048.0, A_.add)
        act("CW", P(6, 1), F_.Relu, -1.0)
        mms(P(4, 1), ("I", "KA"), ("NI", "DW"), ("TR", "DO"))
        act("KA", P(4, 1), F_.Relu)
        act("XH", IND(WD, X("ll")), F_.Copy)
        mms(P(0, 1), ("I", "W2"), ("NI", "W1"), ("B", "CO"))
        wrap(X("b6", 32, 48), "CW")
        mms(P(3, 1), ("HALF", "XG"), ("HALF", "XH"))
        act("W2G", P(0, 1), F_.Relu, 1.0, -1.0)
        tt("ye2", "p2", "dum", A_.add)
        ts("yel", "ye2", 16.0, A_.mult)
        if fin:
            ts("XI", P(3, 1), -0.25, A_.add)
        if last:
            mms(P(5, 1), ("IR", "KA"))
            mms(P(7, 1), ("I", qc), ("I2K", "ONES"))
            leave(rnd)
        else:
            mms(P(5, 1), ("B", "OA"), ("BN4", "LO"), ("BN4", "CO"), ("ISH", "KA"))
            act("OA", P(5, 1), F_.Relu, 1.0, -1.0)
        if fin:
            edges_out(base, qc)
            cp(X("E", 0, 1), X("save", 0, 1))
            dma("y", "d7", T.ye[:], T.E[:, 0:1856], [("E", 0, 1856, 1)], [])
        tt("px", "qmd", X("b6", 32, 48), A_.mult)
        tt("yx2", "px", "dumx", A_.add)
        if not fin:
            ts("XI", P(3, 1), -0.25, A_.add)
        ts("yxl", "yx2", 2048.0, A_.add)
        cp(IND(WDS, X("yxl")), "XI")
        if fin:
            cp(X("D", 4095, 4096), X("savd", 15, 16))
            dma("y", "d6", T.yd[:], T.D[:, 0:4096], [("D", 0, 4096, 1)], [])
            return
        wl = X("b6", 48, 64)
        wrap(wl, "LO")
        mms(P(0, 0), (X("IF"), "CV"), ("BP4K", "LO"), ("IN4K", "W1"))
        act("VA", P(0, 0), F_.Relu, 1.0, -4096.0)
        gq(0, "LQ1" if last else lst)
        mms(P(2, 0), ("I", "LC"), ("TRN4K", "CO"), ("K6", "ONES"))
        mms(P(4, 0), ("I", "NA%d" % rnd), ("I2K", "W1"), ("I2K", "W2G"), ("I", "W2G"))
        act("NV", P(4, 0), F_.Copy)
        for c in range(1, 4):
            gq(c, "LQ1" if last else lst)
        tt("p1", "vmd", wl, A_.mult)
        if not last:
            tt("TP", "OA", P(1, 1), A_.mult)
            mms(P(7, 0), ("I", "VB"), ("I", "EV"), ("BN1K", "OA"))
            mms(P(0, 1), ("B", "TP"))
        tt("yc2", "ye2", "p1", A_.add)
        ts(IND(WES, X("yel")), "EC", -1.0, A_.mult, 4095.0, A_.add)
        ts("ycl", "yc2", 16.0, A_.mult)
        if not last:
            ts("VB", P(7, 0), 1024.0, A_.add)
        mms(P(5, 1), ("I", qc), ("TRN4K", "CO"), ("BN4K", "W2G"), ("K10", "ONES"))
        if not last:
            wrap(W0, "VB")
        mms(P(4, 1), ("I", qc), ("TRN4K", "LO"), ("K6", "ONES"))
        if not last:
            ts("OT", P(0, 1), PM, A_.is_equal, 1.0 / 16, A_.mult)
        else:
            prep("LQ1", "QC1", "QH1")
        ev, od = X("E", base, base + 512, 2), X("E", base + 1, base + 512, 2)
        tt(ev, ev, P(2, 0), A_.min)
        mms(P(7, 1), (X("IF"), "CC"), ("BP4K", "CO"), ("IN4K", "ONES"))
        tt(IND(WCS, X("ycl")), "VA", "NV", A_.max)
        tt(od, od, P(5, 1), A_.min)
        if not last:
            ts("vl", W0, 1855.0, A_.min)
            ts("vs", W0, 1.0 / 16, A_.mult)
        tt(ev, ev, P(4, 1), A_.min)
        cn = X("C", base, base + 512, 2)
        tt(cn, cn, P(7, 1), A_.max)
        if last:
            roots("QC1", "QH1")
            qres("QC1", "QH1")

    def edges_out(base, qc):
        mms(P(2, 0), ("I", "LC"), ("TRN4K", "CO"), ("K6", "ONES"))
        mms(P(4, 1), ("I", qc), ("TRN4K", "LO"), ("K6", "ONES"))
        mms(P(5, 1), ("I", qc), ("TRN4K", "CO"), ("BN4K", "W2G"), ("K10", "ONES"))
        ts(IND(WES, X("yel")), "EC", -1.0, A_.mult, 4095.0, A_.add)
        ev, od = X("E", base, base + 512, 2), X("E", base + 1, base + 512, 2)
        tt(ev, ev, P(2, 0), A_.min)
        tt(od, od, P(5, 1), A_.min)
        tt(ev, ev, P(4, 1), A_.min)

    cp("QU", "qin")
    prep("QU", "QC0", "QH0")
    ts("dum", "dum", PM, A_.add)
    ts("dum", "dum", 1.0 / 16, A_.mult)
    roots("QC0", "QH0")
    qres("QC0", "QH0")
    cp(X("C", 0, 832), "cin")
    cp(X("D", 4080, 4096), "savd")
    fill(X("D", 4095, 4096), 20000.0)
    for c in range(4):
        gq(c, "QU")
    for rnd in range(2):
        lst, qc = ("QU", "LQ1")[rnd], "QC%d" % rnd
        for s in range(3):
            walk(rnd, s, lst, qc)
            decide(rnd, s, lst, qc)
    dma("y", "d5", T.yr[:, 64:256], T.YRL[:, 64:256], [("YRL", 64, 256, 1)], [])
    finish("y")
